import numpy as np, ml_dtypes
CORES = [83,85,87,115,117,119]
N = 6
BF = ml_dtypes.bfloat16
def gentries(a):
    return np.ascontiguousarray(a.reshape(8, 16, -1).transpose(0, 2, 1)).reshape(8, -1)
def gtable(e):
    e = np.asarray(e); return np.ascontiguousarray(e.reshape(8, -1, 16).transpose(0, 2, 1)).reshape(128, -1).astype(np.int32)
V, DV, M, DC, IT, CAP, B = 192, 3, 144, 4, 2, 128, 63
E = V * DV
def mixed(rng):
    c = np.full((N, N), E // N)
    for i in range(6 * N):
        p, p2 = rng.permutation(N)[:2]; q, q2 = rng.permutation(N)[:2]
        t = rng.integers(0, min(c[p, q2], c[p2, q], CAP - c[p, q], CAP - c[p2, q2]) + 1)
        c[p, q] += t; c[p2, q2] += t; c[p, q2] -= t; c[p2, q] -= t
    return c
def fullest(rng):
    odd = np.add.outer(rng.permutation(N), rng.permutation(N)) % 2
    return E // N + (CAP - E // N) * (1 - 2 * odd)
def fewest(rng):
    low = max(0, E - (N - 1) * CAP); each = (E - low) // (N - 1); more = E - low - each * (N - 1)
    w = np.concatenate([[low], each + (np.arange(N - 1) < more)]); k = rng.integers(1, N); p = np.arange(N)
    c = np.zeros((N, N), np.int64)
    for i in range(N): c[p, (p + k + i) % N] = w[i]
    return c
def graph(rng, ways, near=False, holes=False):
    sn = rng.integers(0, V, (N, 8, N * CAP)); pl = np.zeros((N, 8, E), np.int64); vl = np.zeros((N, 8, E), np.int64)
    def order(n, d):
        return np.add.outer(rng.permutation(n), n * np.arange(d)).reshape(-1) if near else rng.permutation(n * d)
    ve = [[order(V, DV) for r in range(N)] for g in range(8)]; ce = [[order(M, DC) for r in range(N)] for g in range(8)]
    c = ways(rng); va = np.add.accumulate(c, axis=1) - c; ca = np.add.accumulate(c, axis=0) - c
    for g in range(8):
        for p in range(N):
            for q in range(N):
                h = (g + p * q) % 8; n = int(c[p, q]); s = rng.permutation(CAP if holes else n)[:n]
                a = ve[g][p][va[p, q]:va[p, q] + n]; b = ce[h][q][ca[p, q]:ca[p, q] + n]
                vl[p, g, a] = q * CAP + s; pl[q, h, b] = p * CAP + s; sn[p, g, q * CAP + s] = a % V
    return {"sn": np.stack([gtable(e) for e in sn]), "pl": np.stack([gtable(e) for e in pl]), "vl": np.stack([gtable(e) for e in vl])}
def heard(rng):
    k = np.stack([rng.permutation(16) for g in range(8)]).reshape(1, 128, 1)
    mean = B * np.array([0, 0.1, 0.2, 0.7])[k // 4]; noise = B * np.array([0.1, 0.2, 0.4, 0.6])[k % 4]
    return (np.clip(np.rint(mean + noise * rng.standard_normal((N, 128, V))), -B, B) + 0.0).astype(BF)
def setup_inputs(rng):
    return {"x": heard(rng), **graph(rng, mixed)}
def setup_inputs_full(rng):
    return {"x": heard(rng), **graph(rng, fullest)}
def setup_inputs_holes(rng):
    return {"x": heard(rng), **graph(rng, fewest, holes=True)}
def setup_inputs_ties(rng):
    k = np.stack([rng.permutation(16) for g in range(8)]).reshape(1, 128, 1) % 4; z = (N, 128, V)
    sg = 2 * rng.integers(0, 2, z) - 1
    v = np.where(k == 0, sg, np.where(k == 1, rng.integers(-2, 3, z), np.where(k == 2, np.where(rng.random(z) < 0.1, -B, B), np.where(rng.random(z) < 0.0625, 0, B * sg))))
    return {"x": v.astype(BF), **graph(rng, mixed)}
def setup_inputs_twins(rng):
    return {"x": heard(rng), **graph(rng, mixed, near=True)}
def setup_inputs_spread(rng):
    hi = B >> rng.integers(0, 6, (N, 128, 1)); hi[:, ::16] = B
    v = rng.integers(-hi, hi + 1, (N, 128, V)) * (rng.random((N, 1, V)) > 0.0625)
    return {"x": v.astype(BF), **graph(rng, mixed, holes=True)}
def check_inputs(d):
    bad = []
    try:
        x = np.asarray(d["x"]).astype(np.float64)
        if not (np.isfinite(x).all() and (x == np.rint(x)).all() and (np.abs(x) <= B).all()): bad.append("x is whole and within B")
        sn, pl, vl = [np.stack([gentries(np.asarray(d[k][r])) for r in range(N)]).astype(np.int64) for k in ("sn", "pl", "vl")]
        if sn.min() < 0 or sn.max() >= V: bad.append("sn in range")
        if min(pl.min(), vl.min()) < 0 or max(pl.max(), vl.max()) >= N * CAP: return bad + ["pl and vl in range"]
        name = True; v = np.arange(E) % V
        uv = np.zeros((8, N, N * CAP), np.int64); uc = np.zeros((8, N, N * CAP), np.int64)
        for g in range(8):
            for r in range(N):
                uv[g, r] = np.bincount(vl[r, g], minlength=N * CAP); uc[g, r] = np.bincount(pl[r, g], minlength=N * CAP)
                name = name and bool((sn[r, g][vl[r, g]] == v).all())
        a = np.arange(N); h = (np.arange(8)[:, None, None] + np.multiply.outer(a, a)) % 8
        there = uc.reshape(8, N, N, CAP).transpose(0, 2, 1, 3)[h, a[:, None], a] > 0
        if max(uv.max(), uc.max()) > 1: bad.append("entries of pl and of vl differ")
        if not ((uv.reshape(8, N, N, CAP) > 0) == there).all(): bad.append("vl and pl name the same slots")
        if not name: bad.append("sn names the variable of each slot")
    except Exception:
        bad.append("shapes")
    return bad
def reference(x, sn, pl, vl):
    g = np.arange(8)[:, None, None]; r = np.arange(N)[:, None]
    ve = np.stack([gentries(vl[p]).astype(np.int64) for p in range(N)], axis=1) + (g * N + r) * N * CAP
    k = np.stack([gentries(pl[q]).astype(np.int64) for q in range(N)], axis=1); p = k // CAP
    ce = (((g - p * r) % 8 * N + p) * N + r) * CAP + k % CAP
    u = x.astype(np.float32).astype(np.int64).reshape(N, 8, 16, V).transpose(2, 1, 0, 3)
    back = np.zeros((16, 8 * N * N * CAP), np.int64); there = np.zeros((16, 8 * N * N * CAP), np.int64); tot = u
    for i in range(IT):
        there[:, ve] = np.clip(np.tile(tot, (1, 1, 1, DV)) - back[:, ve], -B, B)
        m = there[:, ce].reshape(16, 8, N, DC, M); size = np.abs(m); neg = (m < 0).astype(np.int64); new = np.zeros_like(m)
        for e in range(DC):
            o = [j for j in range(DC) if j != e]
            new[:, :, :, e] = np.min(size[:, :, :, o], axis=3) * (1 - 2 * (np.add.reduce(neg[:, :, :, o], axis=3) % 2))
        back[:, ce] = new.reshape(16, 8, N, E)
        tot = u + np.add.reduce(back[:, ve].reshape(16, 8, N, DV, V), axis=3)
    return {"y": np.ascontiguousarray(tot.transpose(2, 1, 0, 3)).reshape(N, 128, V).astype(np.float32)}

@@ -1,0 +1,276 @@
+from concourse.bass import DstId, RemoteDMATransfer
+from concourse.mybir import AluOpType, ActivationFunctionType
+
+N, CAP, V, M, IT = 6, 128, 192, 144, 2
+SL = N * CAP
+E = 576
+Act = ActivationFunctionType
+Op = AluOpType
+
+SCRATCH = {
+    "x_sb": ("sbuf", [128, V], "bfloat16"),
+    "sn_i": ("sbuf", [128, 48], "int32"),
+    "pl_i": ("sbuf", [128, 36], "int32"),
+    "vl_i": ("sbuf", [128, 36], "int32"),
+    "sn16": ("sbuf", [128, 48], "uint16"),
+    "pl16": ("sbuf", [128, 36], "uint16"),
+    "vl16": ("sbuf", [128, 36], "uint16"),
+    "inv16": ("sbuf", [128, 48], "uint16"),
+    "ones": ("sbuf", [128, 256], "bfloat16"),
+    "W": ("sbuf", [128, 256], "bfloat16"),
+    "Wn": ("sbuf", [128, 256], "bfloat16"),
+    "I16": ("sbuf", [128, 128], "float16"),
+    "ri": ("sbuf", [128, 16], "int32"),
+    "ri2": ("sbuf", [128, 16], "int32"),
+    "mask": ("sbuf", [128, 16], "float32"),
+    "jota": ("sbuf", [128, E], "float32"),
+    "win": ("sbuf", [128, SL], "float32"),
+    "mk": ("sbuf", [128, SL], "float16"),
+    "ysb": ("sbuf", [128, V], "float32"),
+}
+for _k in range(IT):
+    SCRATCH["gf%d" % _k] = ("sbuf", [128, SL], "bfloat16")
+    SCRATCH["sf%d" % _k] = ("sbuf", [128, SL], "bfloat16")
+    SCRATCH["lf%d" % _k] = ("sbuf", [128, SL], "bfloat16")
+    SCRATCH["gb%d" % _k] = ("sbuf", [128, SL], "bfloat16")
+    SCRATCH["sb%d" % _k] = ("sbuf", [128, SL], "bfloat16")
+    SCRATCH["lb%d" % _k] = ("sbuf", [128, SL], "bfloat16")
+    SCRATCH["A%d" % _k] = ("sbuf", [128, E], "bfloat16")
+    SCRATCH["G%d" % _k] = ("sbuf", [128, E], "bfloat16")
+    SCRATCH["S%d" % _k] = ("sbuf", [128, E], "bfloat16")
+    SCRATCH["R%d" % _k] = ("sbuf", [128, E], "bfloat16")
+    SCRATCH["par%d" % _k] = ("sbuf", [128, M], "bfloat16")
+    SCRATCH["ta%d" % _k] = ("sbuf", [128, V], "bfloat16")
+    SCRATCH["tb%d" % _k] = ("sbuf", [128, V], "bfloat16")
+    SCRATCH["tc%d" % _k] = ("sbuf", [128, V], "bfloat16")
+for _k in range(8):
+    SCRATCH["bank%d" % _k] = ("psum", [128, 512], "float32")
+
+NS = 140
+SEMAPHORES = ["arr%d" % k for k in range(4)] + ["sent"] + ["s%d" % k for k in range(NS)]
+
+
+def rank_program(g, core, T, topo):
+    p = T.rank_of(core)
+    if p is None:
+        return
+    cores = list(T.cores)
+    v, s, t, sy = g.vector, g.scalar, g.tensor, g.sync
+
+    tot, seen, nxt = {}, {}, [0]
+
+    def new():
+        n = "s%d" % nxt[0]
+        nxt[0] += 1
+        return n
+
+    def inc(ins, name, n=1):
+        ins.then_inc(T.sem[name], n)
+        tot[name] = tot.get(name, 0) + n
+        return name
+
+    def need(queue, qname, *names):
+        for name in names:
+            if seen.get((qname, name), 0) < tot[name]:
+                queue.wait_ge(T.sem[name], tot[name])
+                seen[(qname, name)] = tot[name]
+
+    def col(q):
+        return slice(q * CAP, (q + 1) * CAP)
+
+    off = [q for q in range(N) if topo.chip(cores[q]) != topo.chip(core)]
+    on = [q for q in range(N) if topo.chip(cores[q]) == topo.chip(core) and q != p]
+    order = off + on + [p]
+
+    def pow2(n):
+        k = 1
+        while 2 * k <= n:
+            k *= 2
+        return k
+
+    off_eng = topo.engines(core, cores[off[0]])
+    on_eng = [e for e in topo.engines(core, cores[on[0]]) if e not in off_eng]
+    off_per, on_per = pow2(len(off_eng) // len(off)), pow2(len(on_eng) // len(on))
+    emask = {}
+    for lst, eng, per in ((off, off_eng, off_per), (on, on_eng, on_per)):
+        for i, q in enumerate(lst):
+            emask[q] = sum(1 << e for e in eng[i * per:(i + 1) * per])
+
+    def send(k, src, dst, qs):
+        trs = []
+        for q in qs:
+            rid, pid, _ = topo.addr(cores[q])
+            trs.append(RemoteDMATransfer(dst_ids=[DstId(rid=rid, pnc=pid)], dma_engine_mask=emask[q],
+                                         remote_sem=T.sem["arr%d" % k], src=src[:, col(q)], dst=dst[:, col(p)]))
+            tot["sent"] = tot.get("sent", 0) + bin(emask[q]).count("1")
+        g.remote_dma_fused(trs, local_sem=T.sem["sent"])
+
+    arrive = len(off) * off_per + len(on) * on_per
+    for k in range(4):
+        tot["arr%d" % k] = arrive
+
+    lsn, lx, lpl, lvl = new(), new(), new(), new()
+    inc(sy.dma_start(T.sn_i[:], T.sn[:]), lsn, 16)
+    inc(s.dma_start(T.x_sb[:], T.x[:]), lx, 16)
+    inc(sy.dma_start(T.pl_i[:], T.pl[:]), lpl, 16)
+    inc(sy.dma_start(T.vl_i[:], T.vl[:]), lvl, 16)
+
+    kones = inc(v.memset(T.ones[:], 1.0), new())
+    kwin = inc(v.memset(T.win[:], 0.0), new())
+    need(g, "g", kones)
+    kW = inc(g.affine_select(T.W[:], T.ones[:], [[0, 2], [-1, 128]], Op.is_equal, 0.0, 0, 1), new())
+    kri = inc(g.iota(T.ri[:], [[-1, 16]], 128, 1), new())
+    kj = inc(g.iota(T.jota[:], [[1, E]], 0, 0, allow_small_or_imprecise_dtypes=True), new())
+
+    def turn(r, neg=False):
+        o = 128 - 16 * (r % 8)
+        return (T.Wn if neg else T.W)[:, o:o + 128]
+
+    banks = [T["bank%d" % i] for i in range(8)]
+    bank_read = [[] for _ in range(8)]
+    ident = T.W[:, 0:128]
+
+    def exchange(k, window, lists, ready, gbuf, sbuf, lbuf, sign, minus=None, clip=False):
+        started = {}
+        if minus is not None:
+            need(t, "t", *minus[1])
+            for i, q in enumerate(order):
+                need(t, "t", *bank_read[i])
+                t.matmul(banks[i][:, 0:128], turn(sign * p * q, True), minus[0][:, col(q)], True, False)
+                started[i] = True
+        gs = {}
+
+        def gather(who, i):
+            q = order[i]
+            o, w = gbuf[:, col(q)], window.indirect(lists[:, 8 * q:8 * q + 8])
+            if who == "v":
+                need(v, "v", *ready)
+                if clip:
+                    ins = v.tensor_scalar(o, w, 63.0, -63.0, Op.min, Op.max)
+                else:
+                    ins = v.tensor_copy(o, w)
+            else:
+                need(s, "s", *ready)
+                ins = s.activation(o, w, Act.Copy)
+            gs[i] = inc(ins, new())
+
+        ms = {}
+
+        def mm(i):
+            q = order[i]
+            need(t, "t", gs[i], kW, *bank_read[i])
+            ms[i] = inc(t.matmul(banks[i][:, 0:128], turn(sign * p * q), gbuf[:, col(q)], i not in started, True), new())
+
+        e_off, e_on, e_own = new(), new(), new()
+
+        def out(who, i):
+            q = order[i]
+            o = (lbuf if q == p else sbuf)[:, col(q)]
+            sem = e_off if i < len(off) else (e_own if q == p else e_on)
+            b = banks[i][:, 0:128]
+            if who == "v":
+                need(v, "v", ms[i])
+                if clip:
+                    ins = v.tensor_scalar(o, b, 63.0, -63.0, Op.min, Op.max)
+                else:
+                    ins = v.tensor_copy(o, b)
+            else:
+                need(s, "s", ms[i])
+                ins = s.activation(o, b, Act.Copy)
+            inc(ins, sem)
+            bank_read[i] = [sem]
+
+        gather("v", 0); gather("s", 1); mm(0); mm(1)
+        gather("v", 2); mm(2); out("s", 0); out("v", 1)
+        gather("s", 3); out("s", 2); mm(3)
+        gather("v", 4); mm(4); gather("s", 5); mm(5)
+        out("v", 3); out("s", 4); out("v", 5)
+        need(g, "g", e_off)
+        send(k, sbuf, lbuf, off)
+        need(g, "g", e_on)
+        send(k, sbuf, lbuf, on)
+        return [e_own, "arr%d" % k]
+
+    need(v, "v", lsn)
+    ksn = inc(v.tensor_copy(T.sn16[:], T.sn_i[:]), new())
+    here = exchange(0, T.x_sb[:, 0:V], T.sn16, [ksn, lx], T.gf0, T.sf0, T.lf0, 1)
+
+    need(v, "v", lpl)
+    kpl = inc(v.tensor_copy(T.pl16[:], T.pl_i[:]), new())
+    need(v, "v", kri)
+    k1 = inc(v.tensor_scalar(T.ri2[:], T.ri[:], 15, None, Op.bitwise_and), new())
+    need(v, "v", kpl, kj, kwin)
+    ksc = inc(v.tensor_copy(T.win[:].indirect(T.pl16[:, 0:36]), T.jota[:]), new())
+    need(v, "v", k1)
+    kmask = inc(v.tensor_scalar(T.mask[:], T.ri2[:], 0.0, None, Op.is_equal), new())
+    need(v, "v", kW)
+    kI = inc(v.tensor_copy(T.I16[:], T.W[:, 0:128]), new())
+    need(v, "v", ksc, kmask)
+    km = [new(), new()]
+    for r in range(16):
+        inc(v.tensor_scalar(T.mk[:, 48 * r:48 * r + 48], T.win[:, r::16], T.mask[:, r:r + 1], None, Op.mult), km[r // 8])
+    kinvs = new()
+    for r in range(16):
+        need(t, "t", kI, km[r // 8]) if r % 8 == 0 else None
+        ins = t.matmul(banks[7][:, 0:48], T.I16[:], T.mk[:, 48 * r:48 * r + 48], r == 0, r == 15)
+    inc(ins, kinvs)
+    need(v, "v", lvl)
+    kvl = inc(v.tensor_copy(T.vl16[:], T.vl_i[:]), new())
+    kWn = inc(v.tensor_scalar(T.Wn[:], T.W[:], -1.0, None, Op.mult), new())
+    need(v, "v", kinvs)
+    kinv = inc(v.tensor_copy(T.inv16[:], banks[7][:, 0:48]), new())
+    bank_read[7] = [kinv]
+
+    for k in range(IT):
+        lf, lb = T["lf%d" % k], T["lb%d" % k]
+        A, G, S, R, par = [T["%s%d" % (n, k)] for n in ("A", "G", "S", "R", "par")]
+        need(s, "s", kpl, *here)
+        kA = inc(s.activation(A[:], lf[:].indirect(T.pl16[:, 0:36]), Act.Abs, 0.0, 4.0), new())
+        need(v, "v", kpl, *here)
+        kG = inc(v.tensor_scalar(G[:], lf[:].indirect(T.pl16[:, 0:36]), 0.0, 0.5, Op.is_ge, Op.subtract), new())
+        need(t, "t", kG, *bank_read[6])
+        for e in range(4):
+            ins = t.matmul(banks[6][:, 0:M], ident, G[:, e * M:(e + 1) * M], e == 0, e == 3)
+        kN = inc(ins, new())
+        need(s, "s", kN)
+        kpar = inc(s.activation(par[:], banks[6][:, 0:M], Act.Abs), new())
+        bank_read[6] = [kpar]
+        bp, bx, bg = banks[5], (banks[1], banks[3]), banks[7]
+        need(v, "v", kA, *bank_read[5])
+        kP = new()
+        inc(v.tensor_tensor(bp[:, M:2 * M], A[:, 0:M], A[:, 2 * M:3 * M], Op.min), kP)
+        inc(v.tensor_tensor(bp[:, 0:M], A[:, M:2 * M], A[:, 3 * M:4 * M], Op.min), kP)
+        need(v, "v", kP)
+        kS = new()
+        inc(v.tensor_tensor(S[:, 0:2 * M], A[:, 2 * M:4 * M], bp[:, 0:2 * M], Op.min), kS)
+        inc(v.tensor_tensor(S[:, 2 * M:4 * M], A[:, 0:2 * M], bp[:, 0:2 * M], Op.min), kS)
+        need(v, "v", kpar, *bank_read[7])
+        kg = inc(v.tensor_scalar(bg[:, 0:M], par[:], 1.0, 0.5, Op.not_equal, Op.subtract), new())
+        need(v, "v", kS, kg, *(bank_read[1] + bank_read[3]))
+        kX = new()
+        for e in range(4):
+            b = bx[e // 2][:, (e % 2) * M:(e % 2 + 1) * M]
+            inc(v.tensor_tensor(b, S[:, e * M:(e + 1) * M], bg[:, 0:M], Op.mult), kX)
+        need(v, "v", kX)
+        kR = new()
+        for h in range(2):
+            inc(v.tensor_tensor(R[:, 2 * h * M:2 * (h + 1) * M], G[:, 2 * h * M:2 * (h + 1) * M], bx[h][:, 0:2 * M], Op.mult), kR)
+        bank_read[5], bank_read[7], bank_read[1], bank_read[3] = [kS], [kX], [kR], [kR]
+        here = exchange(2 * k + 1, R[:], T.inv16, [kinv, kR], T["gb%d" % k], T["sb%d" % k], lb, -1, clip=k == IT - 1)
+        last = k == IT - 1
+        need(v, "v", kvl, lx, *here)
+        prev = T.x_sb
+        outs = [T["ta%d" % k], T["tb%d" % k], T.ysb if last else T["tc%d" % k]]
+        for d in range(3):
+            kT = inc(v.tensor_tensor(outs[d][:], lb[:].indirect(T.vl16[:, 12 * d:12 * d + 12]), prev[:], Op.add), new())
+            prev = outs[d]
+            if d < 2:
+                need(v, "v", kT)
+        if not last:
+            here = exchange(2, prev[:, 0:V], T.sn16, [kT], T.gf1, T.sf1, T.lf1, 1, minus=(lb, [kWn] + here))
+    need(sy, "sy", kT)
+    kst = inc(sy.dma_start(T.y[:], T.ysb[:]), new(), 16)
+
+    for name in sorted(tot):
+        if max([n for (_, m), n in seen.items() if m == name] + [0]) < tot[name]:
+            need(g, "g", name)

@@ -4,6 +4,8 @@ from concourse.mybir import AluOpType, ActivationFunctionType
 N, CAP, V, M, IT = 6, 128, 192, 144, 2
 SL = N * CAP
 E = 576
+HALF = (80, 64)
+VA = 128
 Act = ActivationFunctionType
 Op = AluOpType
 
@@ -15,6 +17,7 @@ SCRATCH = {
     "sn16": ("sbuf", [128, 48], "uint16"),
     "pl16": ("sbuf", [128, 36], "uint16"),
     "vl16": ("sbuf", [128, 36], "uint16"),
+    "vs16": ("sbuf", [128, 12], "uint16"),
     "inv16": ("sbuf", [128, 48], "uint16"),
     "ones": ("sbuf", [128, 256], "bfloat16"),
     "W": ("sbuf", [128, 256], "bfloat16"),
@@ -27,6 +30,7 @@ SCRATCH = {
     "win": ("sbuf", [128, SL], "float32"),
     "mk": ("sbuf", [128, SL], "float16"),
     "ysb": ("sbuf", [128, V], "float32"),
+    "tot": ("sbuf", [128, V], "bfloat16"),
 }
 for _k in range(IT):
     SCRATCH["gf%d" % _k] = ("sbuf", [128, SL], "bfloat16")
@@ -35,18 +39,19 @@ for _k in range(IT):
     SCRATCH["gb%d" % _k] = ("sbuf", [128, SL], "bfloat16")
     SCRATCH["sb%d" % _k] = ("sbuf", [128, SL], "bfloat16")
     SCRATCH["lb%d" % _k] = ("sbuf", [128, SL], "bfloat16")
+    SCRATCH["sg%d" % _k] = ("sbuf", [128, SL], "bfloat16")
     SCRATCH["A%d" % _k] = ("sbuf", [128, E], "bfloat16")
     SCRATCH["G%d" % _k] = ("sbuf", [128, E], "bfloat16")
     SCRATCH["S%d" % _k] = ("sbuf", [128, E], "bfloat16")
-    SCRATCH["R%d" % _k] = ("sbuf", [128, E], "bfloat16")
+    SCRATCH["X%d" % _k] = ("sbuf", [128, E], "bfloat16")
     SCRATCH["par%d" % _k] = ("sbuf", [128, M], "bfloat16")
-    SCRATCH["ta%d" % _k] = ("sbuf", [128, V], "bfloat16")
-    SCRATCH["tb%d" % _k] = ("sbuf", [128, V], "bfloat16")
-    SCRATCH["tc%d" % _k] = ("sbuf", [128, V], "bfloat16")
+    SCRATCH["ta%d" % _k] = ("sbuf", [128, VA], "bfloat16")
+    SCRATCH["tb%d" % _k] = ("sbuf", [128, VA], "bfloat16")
+    SCRATCH["rs%d" % _k] = ("sbuf", [128, 3 * (V - VA)], "bfloat16")
 for _k in range(8):
     SCRATCH["bank%d" % _k] = ("psum", [128, 512], "float32")
 
-NS = 140
+NS = 144
 SEMAPHORES = ["arr%d" % k for k in range(4)] + ["sent"] + ["s%d" % k for k in range(NS)]
 
 
@@ -78,34 +83,32 @@ def rank_program(g, core, T, topo):
     def col(q):
         return slice(q * CAP, (q + 1) * CAP)
 
-    off = [q for q in range(N) if topo.chip(cores[q]) != topo.chip(core)]
-    on = [q for q in range(N) if topo.chip(cores[q]) == topo.chip(core) and q != p]
+    def plan(r):
+        me = cores[r]
+        near = [q for q in range(N) if topo.chip(cores[q]) == topo.chip(me)]
+        far = [q for q in range(N) if q not in near]
+        k = near.index(r)
+        far = [far[(i + k) % len(far)] for i in range(len(far))]
+        on = [near[(i + k) % len(near)] for i in range(1, len(near))]
+        fe = topo.engines(me, cores[far[0]])
+        ne = [e for e in topo.engines(me, cores[on[0]]) if e not in fe]
+        h, m = len(fe) // 2, len(ne) // 2
+        eng = {far[0]: fe[:h], far[1]: fe[h:], far[2]: fe, on[0]: ne[:m], on[1]: ne[m:]}
+        return far, on, eng
+
+    off, on, eng = plan(p)
     order = off + on + [p]
-
-    def pow2(n):
-        k = 1
-        while 2 * k <= n:
-            k *= 2
-        return k
-
-    off_eng = topo.engines(core, cores[off[0]])
-    on_eng = [e for e in topo.engines(core, cores[on[0]]) if e not in off_eng]
-    off_per, on_per = pow2(len(off_eng) // len(off)), pow2(len(on_eng) // len(on))
-    emask = {}
-    for lst, eng, per in ((off, off_eng, off_per), (on, on_eng, on_per)):
-        for i, q in enumerate(lst):
-            emask[q] = sum(1 << e for e in eng[i * per:(i + 1) * per])
+    arrive = sum(len(plan(r)[2][p]) for r in range(N) if r != p)
 
     def send(k, src, dst, qs):
         trs = []
         for q in qs:
             rid, pid, _ = topo.addr(cores[q])
-            trs.append(RemoteDMATransfer(dst_ids=[DstId(rid=rid, pnc=pid)], dma_engine_mask=emask[q],
+            trs.append(RemoteDMATransfer(dst_ids=[DstId(rid=rid, pnc=pid)], dma_engine_mask=sum(1 << e for e in eng[q]),
                                          remote_sem=T.sem["arr%d" % k], src=src[:, col(q)], dst=dst[:, col(p)]))
-            tot["sent"] = tot.get("sent", 0) + bin(emask[q]).count("1")
+            tot["sent"] = tot.get("sent", 0) + len(eng[q])
         g.remote_dma_fused(trs, local_sem=T.sem["sent"])
 
-    arrive = len(off) * off_per + len(on) * on_per
     for k in range(4):
         tot["arr%d" % k] = arrive
 
@@ -121,6 +124,13 @@ def rank_program(g, core, T, topo):
     kW = inc(g.affine_select(T.W[:], T.ones[:], [[0, 2], [-1, 128]], Op.is_equal, 0.0, 0, 1), new())
     kri = inc(g.iota(T.ri[:], [[-1, 16]], 128, 1), new())
     kj = inc(g.iota(T.jota[:], [[1, E]], 0, 0, allow_small_or_imprecise_dtypes=True), new())
+    need(v, "v", kW)
+    kI = inc(v.tensor_copy(T.I16[:], T.W[:, 0:128]), new())
+    kWn = inc(v.tensor_scalar(T.Wn[:], T.W[:], -1.0, None, Op.mult), new())
+    need(v, "v", kri)
+    k1 = inc(v.tensor_scalar(T.ri2[:], T.ri[:], 15, None, Op.bitwise_and), new())
+    need(v, "v", k1)
+    kmask = inc(v.tensor_scalar(T.mask[:], T.ri2[:], 0.0, None, Op.is_equal), new())
 
     def turn(r, neg=False):
         o = 128 - 16 * (r % 8)
@@ -130,146 +140,177 @@ def rank_program(g, core, T, topo):
     bank_read = [[] for _ in range(8)]
     ident = T.W[:, 0:128]
 
-    def exchange(k, window, lists, ready, gbuf, sbuf, lbuf, sign, minus=None, clip=False):
-        started = {}
-        if minus is not None:
-            need(t, "t", *minus[1])
-            for i, q in enumerate(order):
-                need(t, "t", *bank_read[i])
-                t.matmul(banks[i][:, 0:128], turn(sign * p * q, True), minus[0][:, col(q)], True, False)
-                started[i] = True
-        gs = {}
-
-        def gather(who, i):
+    def exchange(k, gather_v, gather_s, steps, gbuf, sbuf, lbuf, sign, started=(), clip=False):
+        gs, ms, es = {}, {}, [new(), new(), new()]
+        for who, what, i in steps:
             q = order[i]
-            o, w = gbuf[:, col(q)], window.indirect(lists[:, 8 * q:8 * q + 8])
-            if who == "v":
-                need(v, "v", *ready)
-                if clip:
-                    ins = v.tensor_scalar(o, w, 63.0, -63.0, Op.min, Op.max)
-                else:
-                    ins = v.tensor_copy(o, w)
-            else:
-                need(s, "s", *ready)
-                ins = s.activation(o, w, Act.Copy)
-            gs[i] = inc(ins, new())
-
-        ms = {}
-
-        def mm(i):
-            q = order[i]
-            need(t, "t", gs[i], kW, *bank_read[i])
-            ms[i] = inc(t.matmul(banks[i][:, 0:128], turn(sign * p * q), gbuf[:, col(q)], i not in started, True), new())
-
-        e_off, e_on, e_own = new(), new(), new()
-
-        def out(who, i):
-            q = order[i]
+            if what == "g":
+                gs[i] = inc((gather_v if who == "v" else gather_s)(q, gbuf[:, col(q)]), new())
+                need(t, "t", gs[i], kW, *bank_read[i])
+                ms[i] = inc(t.matmul(banks[i][:, 0:128], turn(sign * p * q), gbuf[:, col(q)], i not in started, True), new())
+                continue
             o = (lbuf if q == p else sbuf)[:, col(q)]
-            sem = e_off if i < len(off) else (e_own if q == p else e_on)
             b = banks[i][:, 0:128]
             if who == "v":
                 need(v, "v", ms[i])
-                if clip:
-                    ins = v.tensor_scalar(o, b, 63.0, -63.0, Op.min, Op.max)
-                else:
-                    ins = v.tensor_copy(o, b)
+                ins = v.tensor_scalar(o, b, 63.0, -63.0, Op.min, Op.max) if clip else v.tensor_copy(o, b)
             else:
                 need(s, "s", ms[i])
                 ins = s.activation(o, b, Act.Copy)
+            sem = es[0] if i < 2 else (es[2] if q == p else es[1])
             inc(ins, sem)
             bank_read[i] = [sem]
+        need(g, "g", es[0])
+        send(k, sbuf, lbuf, order[:2])
+        need(g, "g", es[1])
+        send(k, sbuf, lbuf, order[2:5])
+        return [es[2], "arr%d" % k]
 
-        gather("v", 0); gather("s", 1); mm(0); mm(1)
-        gather("v", 2); mm(2); out("s", 0); out("v", 1)
-        gather("s", 3); out("s", 2); mm(3)
-        gather("v", 4); mm(4); gather("s", 5); mm(5)
-        out("v", 3); out("s", 4); out("v", 5)
-        need(g, "g", e_off)
-        send(k, sbuf, lbuf, off)
-        need(g, "g", e_on)
-        send(k, sbuf, lbuf, on)
-        return [e_own, "arr%d" % k]
+    def forward(k, window, ready, steps, started=(), clip=False):
+        def gv(q, o):
+            need(v, "v", *ready)
+            return v.tensor_copy(o, window.indirect(T.sn16[:, 8 * q:8 * q + 8]))
+
+        def gs(q, o):
+            need(s, "s", *ready)
+            return s.activation(o, window.indirect(T.sn16[:, 8 * q:8 * q + 8]), Act.Copy)
+        return exchange(2 * k, gv, gs, steps, T["gf%d" % k], T["sf%d" % k], T["lf%d" % k], 1, started, clip)
 
     need(v, "v", lsn)
     ksn = inc(v.tensor_copy(T.sn16[:], T.sn_i[:]), new())
-    here = exchange(0, T.x_sb[:, 0:V], T.sn16, [ksn, lx], T.gf0, T.sf0, T.lf0, 1)
+    here = forward(0, T.x_sb[:, 0:V], [ksn, lx],
+                   [("v", "g", 0), ("s", "g", 1), ("s", "o", 0), ("v", "g", 2), ("v", "o", 1), ("s", "g", 3), ("s", "o", 2),
+                    ("v", "g", 4), ("v", "o", 3), ("s", "o", 4), ("s", "g", 5), ("v", "o", 5)])
 
     need(v, "v", lpl)
-    kpl = inc(v.tensor_copy(T.pl16[:], T.pl_i[:]), new())
-    need(v, "v", kri)
-    k1 = inc(v.tensor_scalar(T.ri2[:], T.ri[:], 15, None, Op.bitwise_and), new())
+    kpl = new()
+    base, c0, o = [], 0, 0
+    for n in HALF:
+        base.append(o * 16)
+        for e in range(4):
+            inc(v.tensor_copy(T.pl16[:, o:o + n // 16], T.pl_i[:, 9 * e + c0:9 * e + c0 + n // 16]), kpl)
+            o += n // 16
+        c0 += n // 16
     need(v, "v", kpl, kj, kwin)
     ksc = inc(v.tensor_copy(T.win[:].indirect(T.pl16[:, 0:36]), T.jota[:]), new())
-    need(v, "v", k1)
-    kmask = inc(v.tensor_scalar(T.mask[:], T.ri2[:], 0.0, None, Op.is_equal), new())
-    need(v, "v", kW)
-    kI = inc(v.tensor_copy(T.I16[:], T.W[:, 0:128]), new())
     need(v, "v", ksc, kmask)
     km = [new(), new()]
     for r in range(16):
         inc(v.tensor_scalar(T.mk[:, 48 * r:48 * r + 48], T.win[:, r::16], T.mask[:, r:r + 1], None, Op.mult), km[r // 8])
-    kinvs = new()
-    for r in range(16):
-        need(t, "t", kI, km[r // 8]) if r % 8 == 0 else None
-        ins = t.matmul(banks[7][:, 0:48], T.I16[:], T.mk[:, 48 * r:48 * r + 48], r == 0, r == 15)
-    inc(ins, kinvs)
-    need(v, "v", lvl)
-    kvl = inc(v.tensor_copy(T.vl16[:], T.vl_i[:]), new())
-    kWn = inc(v.tensor_scalar(T.Wn[:], T.W[:], -1.0, None, Op.mult), new())
+        if r % 8 == 7:
+            need(t, "t", kI, km[r // 8])
+            for u in range(r - 7, r + 1):
+                ins = t.matmul(banks[7][:, 0:48], T.I16[:], T.mk[:, 48 * u:48 * u + 48], u == 0, u == 15)
+    kinvs = inc(ins, new())
     need(v, "v", kinvs)
     kinv = inc(v.tensor_copy(T.inv16[:], banks[7][:, 0:48]), new())
     bank_read[7] = [kinv]
 
+    kvl = None
     for k in range(IT):
-        lf, lb = T["lf%d" % k], T["lb%d" % k]
-        A, G, S, R, par = [T["%s%d" % (n, k)] for n in ("A", "G", "S", "R", "par")]
-        need(s, "s", kpl, *here)
-        kA = inc(s.activation(A[:], lf[:].indirect(T.pl16[:, 0:36]), Act.Abs, 0.0, 4.0), new())
-        need(v, "v", kpl, *here)
-        kG = inc(v.tensor_scalar(G[:], lf[:].indirect(T.pl16[:, 0:36]), 0.0, 0.5, Op.is_ge, Op.subtract), new())
-        need(t, "t", kG, *bank_read[6])
-        for e in range(4):
-            ins = t.matmul(banks[6][:, 0:M], ident, G[:, e * M:(e + 1) * M], e == 0, e == 3)
-        kN = inc(ins, new())
-        need(s, "s", kN)
-        kpar = inc(s.activation(par[:], banks[6][:, 0:M], Act.Abs), new())
-        bank_read[6] = [kpar]
-        bp, bx, bg = banks[5], (banks[1], banks[3]), banks[7]
-        need(v, "v", kA, *bank_read[5])
-        kP = new()
-        inc(v.tensor_tensor(bp[:, M:2 * M], A[:, 0:M], A[:, 2 * M:3 * M], Op.min), kP)
-        inc(v.tensor_tensor(bp[:, 0:M], A[:, M:2 * M], A[:, 3 * M:4 * M], Op.min), kP)
-        need(v, "v", kP)
-        kS = new()
-        inc(v.tensor_tensor(S[:, 0:2 * M], A[:, 2 * M:4 * M], bp[:, 0:2 * M], Op.min), kS)
-        inc(v.tensor_tensor(S[:, 2 * M:4 * M], A[:, 0:2 * M], bp[:, 0:2 * M], Op.min), kS)
-        need(v, "v", kpar, *bank_read[7])
-        kg = inc(v.tensor_scalar(bg[:, 0:M], par[:], 1.0, 0.5, Op.not_equal, Op.subtract), new())
-        need(v, "v", kS, kg, *(bank_read[1] + bank_read[3]))
-        kX = new()
-        for e in range(4):
-            b = bx[e // 2][:, (e % 2) * M:(e % 2 + 1) * M]
-            inc(v.tensor_tensor(b, S[:, e * M:(e + 1) * M], bg[:, 0:M], Op.mult), kX)
-        need(v, "v", kX)
-        kR = new()
-        for h in range(2):
-            inc(v.tensor_tensor(R[:, 2 * h * M:2 * (h + 1) * M], G[:, 2 * h * M:2 * (h + 1) * M], bx[h][:, 0:2 * M], Op.mult), kR)
-        bank_read[5], bank_read[7], bank_read[1], bank_read[3] = [kS], [kX], [kR], [kR]
-        here = exchange(2 * k + 1, R[:], T.inv16, [kinv, kR], T["gb%d" % k], T["sb%d" % k], lb, -1, clip=k == IT - 1)
         last = k == IT - 1
-        need(v, "v", kvl, lx, *here)
-        prev = T.x_sb
-        outs = [T["ta%d" % k], T["tb%d" % k], T.ysb if last else T["tc%d" % k]]
+        lf, lb, sg = T["lf%d" % k], T["lb%d" % k], T["sg%d" % k]
+        A, G, S, X, par = [T["%s%d" % (n, k)] for n in ("A", "G", "S", "X", "par")]
+        cols = [slice(base[h], base[h] + 4 * HALF[h]) for h in range(2)]
+        lst = [T.pl16[:, base[h] // 16:base[h] // 16 + HALF[h] // 4] for h in range(2)]
+        need(s, "s", kpl, *here)
+        need(v, "v", kpl, *here)
+        kA = [inc(s.activation(A[:, cols[h]], lf[:].indirect(lst[h]), Act.Abs, 0.0, 2.0), new()) for h in range(2)]
+        kG = [inc(v.tensor_scalar(G[:, cols[0]], lf[:].indirect(lst[0]), 0.0, 0.5, Op.is_ge, Op.subtract), new()),
+              inc(s.activation(G[:, cols[1]], lf[:].indirect(lst[1]), Act.Sign, 0.5, 1.0), new())]
+        kpar, ksg = [], [new(), new()]
+        far, near = sorted(off), sorted(on + [p])
+        for h, n in enumerate(HALF):
+            need(t, "t", kG[h], *bank_read[6 + h])
+            for e in range(4):
+                b = base[h] + e * n
+                ins = t.matmul(banks[6 + h][:, 0:n], ident, G[:, b:b + n], e == 0, e == 3)
+            kN = inc(ins, new())
+            need(s, "s", kN)
+            ps = slice(0, n) if h == 0 else slice(HALF[0], M)
+            kpar.append(inc(s.activation(par[:, ps], banks[6 + h][:, 0:n], Act.Abs, 0.0, 1.0 if h == 0 else 0.5), new()))
+            bank_read[6 + h] = [kpar[h]]
+            for q in (far if h == 0 else near)[::3]:
+                w = slice(q * CAP, (q + 3) * CAP)
+                inc(s.activation(sg[:, w], lf[:, w], Act.Sign, 0.5, 1.0), ksg[h])
+        bp, bg = banks[5], banks[3]
+        kS = []
+        for h, n in enumerate(HALF):
+            b, o = base[h], (0, 2 * HALF[0])[h]
+            need(v, "v", kA[h], *bank_read[5])
+            kP = new()
+            inc(v.tensor_tensor(bp[:, o + n:o + 2 * n], A[:, b:b + n], A[:, b + 2 * n:b + 3 * n], Op.min), kP)
+            inc(v.tensor_tensor(bp[:, o:o + n], A[:, b + n:b + 2 * n], A[:, b + 3 * n:b + 4 * n], Op.min), kP)
+            need(v, "v", kP)
+            kS.append(new())
+            inc(v.tensor_tensor(S[:, b:b + 2 * n], A[:, b + 2 * n:b + 4 * n], bp[:, o:o + 2 * n], Op.min), kS[h])
+            inc(v.tensor_tensor(S[:, b + 2 * n:b + 4 * n], A[:, b:b + 2 * n], bp[:, o:o + 2 * n], Op.min), kS[h])
+        kX = new()
+        for h, n in enumerate(HALF):
+            ps = slice(0, n) if h == 0 else slice(HALF[0], M)
+            need(v, "v", kpar[h], *bank_read[3])
+            kg = inc(v.tensor_scalar(bg[:, ps], par[:, ps], 1.0, 0.5, Op.not_equal, Op.subtract), new())
+            need(v, "v", kS[h], kg)
+            for e in range(4):
+                b = base[h] + e * n
+                inc(v.tensor_tensor(X[:, b:b + n], S[:, b:b + n], bg[:, ps], Op.mult), kX)
+        bank_read[5], bank_read[3] = list(kS), [kX]
+
+        def gather_back(q, o):
+            need(v, "v", kX, kinv, ksg[0 if q in off else 1])
+            return v.tensor_tensor(o, X[:].indirect(T.inv16[:, 8 * q:8 * q + 8]), sg[:, col(q)], Op.mult)
+
+        steps = []
+        for i in range(6):
+            steps += [("v", "g", i), ("s", "o", i)]
+        here = exchange(2 * k + 1, gather_back, None, steps, T["gb%d" % k], T["sb%d" % k], lb, -1)
+
+        if kvl is None:
+            need(v, "v", lvl)
+            kvl = inc(v.tensor_copy(T.vl16[:], T.vl_i[:]), new())
+            kvs, n = new(), (V - VA) // 16
+            for d in range(3):
+                inc(v.tensor_copy(T.vs16[:, n * d:n * d + n], T.vl_i[:, 12 * d + VA // 16:12 * d + 12]), kvs)
+        res, rs, nb = T.ysb if last else T.tot, T["rs%d" % k], V - VA
+        need(s, "s", kvs, *here)
+        krs = inc(s.activation(rs[:], lb[:].indirect(T.vs16[:, 0:12]), Act.Copy), new())
+        started = []
+
+        def minus(i):
+            q = order[i]
+            need(t, "t", kWn, *(bank_read[i] + here))
+            t.matmul(banks[i][:, 0:128], turn(p * q, True), lb[:, col(q)], True, False)
+            started.append(i)
+
+        need(t, "t", *bank_read[6])
+        t.matmul(banks[6][:, 0:nb], ident, T.x_sb[:, VA:V], True, False)
+        if not last:
+            minus(0)
+            minus(1)
+        need(t, "t", krs)
         for d in range(3):
-            kT = inc(v.tensor_tensor(outs[d][:], lb[:].indirect(T.vl16[:, 12 * d:12 * d + 12]), prev[:], Op.add), new())
+            ins = t.matmul(banks[6][:, 0:nb], ident, rs[:, nb * d:nb * d + nb], False, d == 2)
+        kt = inc(ins, new())
+        need(s, "s", kt)
+        kTs = inc(s.activation(res[:, VA:V], banks[6][:, 0:nb], Act.Copy), new())
+        bank_read[6] = [kTs]
+        if not last:
+            for i in range(2, 6):
+                minus(i)
+        need(v, "v", kvl, lx, *here)
+        prev, outs = T.x_sb, [T["ta%d" % k], T["tb%d" % k], res]
+        for d in range(3):
+            kT = inc(v.tensor_tensor(outs[d][:, 0:VA], lb[:].indirect(T.vl16[:, 12 * d:12 * d + VA // 16]), prev[:, 0:VA], Op.add),
+                     new())
             prev = outs[d]
             if d < 2:
                 need(v, "v", kT)
         if not last:
-            here = exchange(2, prev[:, 0:V], T.sn16, [kT], T.gf1, T.sf1, T.lf1, 1, minus=(lb, [kWn] + here))
-    need(sy, "sy", kT)
-    kst = inc(sy.dma_start(T.y[:], T.ysb[:]), new(), 16)
+            here = forward(1, res[:, 0:V], [kT, kTs],
+                           [("v", "g", 0), ("s", "g", 1), ("s", "g", 2), ("v", "g", 4), ("v", "o", 0), ("v", "o", 1),
+                            ("s", "g", 3), ("v", "o", 2), ("s", "g", 5), ("v", "o", 4), ("v", "o", 3), ("v", "o", 5)], started, True)
+    need(sy, "sy", kT, kTs)
+    inc(sy.dma_start(T.y[:], T.ysb[:]), new(), 16)
 
     for name in sorted(tot):
         if max([n for (_, m), n in seen.items() if m == name] + [0]) < tot[name]:

@@ -1,4 +1,3 @@
-from concourse.bass import DstId, RemoteDMATransfer
 from concourse.mybir import AluOpType, ActivationFunctionType
 
 N, CAP, V, M, IT = 6, 128, 192, 144, 2
@@ -6,31 +5,40 @@ SL = N * CAP
 E = 576
 HALF = (80, 64)
 VA = 128
+XW = 640
 Act = ActivationFunctionType
 Op = AluOpType
 
+F0 = "bg0 vg1 sg2 vo0 so1 sg3 vg4 so2 vo3 sg5 so4 so5"
+B0 = "bg0 vg1 sg2 vo0 vo1 sg3 so2 vg4 vo3 sg5 so4 vo5"
+F1 = "bg0 sg1 sg2 vg4 vo0 vo1 sg3 vo2 sg5 vo4 vo3 vo5"
+B1 = "vg0 so0 vg1 so1 vg2 so2 vg3 so3 vg4 so4 vg5 so5"
+
 SCRATCH = {
     "x_sb": ("sbuf", [128, V], "bfloat16"),
+    "xa": ("sbuf", [128, V], "bfloat16"),
+    "sx": ("sbuf", [128, V], "bfloat16"),
     "sn_i": ("sbuf", [128, 48], "int32"),
     "pl_i": ("sbuf", [128, 36], "int32"),
     "vl_i": ("sbuf", [128, 36], "int32"),
     "sn16": ("sbuf", [128, 48], "uint16"),
     "pl16": ("sbuf", [128, 36], "uint16"),
-    "vl16": ("sbuf", [128, 36], "uint16"),
-    "vs16": ("sbuf", [128, 12], "uint16"),
+    "va16": ("sbuf", [128, 3 * VA // 16], "uint16"),
+    "vs16": ("sbuf", [128, 3 * (V - VA) // 16], "uint16"),
     "inv16": ("sbuf", [128, 48], "uint16"),
     "ones": ("sbuf", [128, 256], "bfloat16"),
     "W": ("sbuf", [128, 256], "bfloat16"),
     "Wn": ("sbuf", [128, 256], "bfloat16"),
-    "I16": ("sbuf", [128, 128], "float16"),
-    "ri": ("sbuf", [128, 16], "int32"),
-    "ri2": ("sbuf", [128, 16], "int32"),
-    "mask": ("sbuf", [128, 16], "float32"),
-    "jota": ("sbuf", [128, E], "float32"),
-    "win": ("sbuf", [128, SL], "float32"),
-    "mk": ("sbuf", [128, SL], "float16"),
-    "ysb": ("sbuf", [128, V], "float32"),
+    "D": ("sbuf", [128, 2048], "bfloat16"),
+    "jota": ("sbuf", [128, E], "bfloat16"),
+    "win": ("sbuf", [128, SL], "bfloat16"),
+    "ta": ("sbuf", [128, VA], "bfloat16"),
+    "tb": ("sbuf", [128, VA], "bfloat16"),
     "tot": ("sbuf", [128, V], "bfloat16"),
+    "ra": ("sbuf", [128, 3 * VA], "bfloat16"),
+    "ysb": ("sbuf", [128, V], "float32"),
+    "b0": ("sbuf", [128, M], "float32"),
+    "sg1": ("sbuf", [128, SL], "bfloat16"),
 }
 for _k in range(IT):
     SCRATCH["gf%d" % _k] = ("sbuf", [128, SL], "bfloat16")
@@ -39,20 +47,17 @@ for _k in range(IT):
     SCRATCH["gb%d" % _k] = ("sbuf", [128, SL], "bfloat16")
     SCRATCH["sb%d" % _k] = ("sbuf", [128, SL], "bfloat16")
     SCRATCH["lb%d" % _k] = ("sbuf", [128, SL], "bfloat16")
-    SCRATCH["sg%d" % _k] = ("sbuf", [128, SL], "bfloat16")
     SCRATCH["A%d" % _k] = ("sbuf", [128, E], "bfloat16")
     SCRATCH["G%d" % _k] = ("sbuf", [128, E], "bfloat16")
     SCRATCH["S%d" % _k] = ("sbuf", [128, E], "bfloat16")
-    SCRATCH["X%d" % _k] = ("sbuf", [128, E], "bfloat16")
+    SCRATCH["X%d" % _k] = ("sbuf", [128, XW], "bfloat16")
     SCRATCH["par%d" % _k] = ("sbuf", [128, M], "bfloat16")
-    SCRATCH["ta%d" % _k] = ("sbuf", [128, VA], "bfloat16")
-    SCRATCH["tb%d" % _k] = ("sbuf", [128, VA], "bfloat16")
     SCRATCH["rs%d" % _k] = ("sbuf", [128, 3 * (V - VA)], "bfloat16")
 for _k in range(8):
     SCRATCH["bank%d" % _k] = ("psum", [128, 512], "float32")
 
-NS = 144
-SEMAPHORES = ["arr%d" % k for k in range(4)] + ["sent"] + ["s%d" % k for k in range(NS)]
+NS = 138
+SEMAPHORES = ["near%d" % k for k in range(4)] + ["far%d" % k for k in range(4)] + ["sent"] + ["s%d" % k for k in range(NS)]
 
 
 def rank_program(g, core, T, topo):
@@ -83,34 +88,24 @@ def rank_program(g, core, T, topo):
     def col(q):
         return slice(q * CAP, (q + 1) * CAP)
 
-    def plan(r):
-        me = cores[r]
-        near = [q for q in range(N) if topo.chip(cores[q]) == topo.chip(me)]
-        far = [q for q in range(N) if q not in near]
-        k = near.index(r)
-        far = [far[(i + k) % len(far)] for i in range(len(far))]
-        on = [near[(i + k) % len(near)] for i in range(1, len(near))]
-        fe = topo.engines(me, cores[far[0]])
-        ne = [e for e in topo.engines(me, cores[on[0]]) if e not in fe]
-        h, m = len(fe) // 2, len(ne) // 2
-        eng = {far[0]: fe[:h], far[1]: fe[h:], far[2]: fe, on[0]: ne[:m], on[1]: ne[m:]}
-        return far, on, eng
-
-    off, on, eng = plan(p)
+    near = [q for q in range(N) if topo.chip(cores[q]) == topo.chip(core)]
+    far = [q for q in range(N) if q not in near]
+    i0 = near.index(p)
+    off = [far[(i + i0) % len(far)] for i in range(len(far))]
+    on = [near[(i + i0) % len(near)] for i in range(1, len(near))]
     order = off + on + [p]
-    arrive = sum(len(plan(r)[2][p]) for r in range(N) if r != p)
+    fe = topo.engines(core, cores[off[0]])
+    ne = [e for e in topo.engines(core, cores[on[0]]) if e not in fe]
 
-    def send(k, src, dst, qs):
-        trs = []
-        for q in qs:
-            rid, pid, _ = topo.addr(cores[q])
-            trs.append(RemoteDMATransfer(dst_ids=[DstId(rid=rid, pnc=pid)], dma_engine_mask=sum(1 << e for e in eng[q]),
-                                         remote_sem=T.sem["arr%d" % k], src=src[:, col(q)], dst=dst[:, col(p)]))
-            tot["sent"] = tot.get("sent", 0) + len(eng[q])
-        g.remote_dma_fused(trs, local_sem=T.sem["sent"])
+    def send(k, src, dst, q):
+        es = fe if q in off else ne
+        rid, pid, _ = topo.addr(cores[q])
+        g.remote_dma(dst[:, col(p)], src[:, col(q)], T.sem["%s%d" % ("far" if q in off else "near", k)], T.sem["sent"],
+                     pid, rid, sum(1 << e for e in es))
+        tot["sent"] = tot.get("sent", 0) + len(es)
 
     for k in range(4):
-        tot["arr%d" % k] = arrive
+        tot["far%d" % k], tot["near%d" % k] = len(off) * len(fe), len(on) * len(ne)
 
     lsn, lx, lpl, lvl = new(), new(), new(), new()
     inc(sy.dma_start(T.sn_i[:], T.sn[:]), lsn, 16)
@@ -119,18 +114,22 @@ def rank_program(g, core, T, topo):
     inc(sy.dma_start(T.vl_i[:], T.vl[:]), lvl, 16)
 
     kones = inc(v.memset(T.ones[:], 1.0), new())
+    kD0 = inc(v.memset(T.D[:], 0.0), new())
     kwin = inc(v.memset(T.win[:], 0.0), new())
+    for k in range(IT):
+        inc(v.memset(T["X%d" % k][:, 512:XW], 0.0), kwin)
     need(g, "g", kones)
     kW = inc(g.affine_select(T.W[:], T.ones[:], [[0, 2], [-1, 128]], Op.is_equal, 0.0, 0, 1), new())
-    kri = inc(g.iota(T.ri[:], [[-1, 16]], 128, 1), new())
-    kj = inc(g.iota(T.jota[:], [[1, E]], 0, 0, allow_small_or_imprecise_dtypes=True), new())
-    need(v, "v", kW)
-    kI = inc(v.tensor_copy(T.I16[:], T.W[:, 0:128]), new())
-    kWn = inc(v.tensor_scalar(T.Wn[:], T.W[:], -1.0, None, Op.mult), new())
-    need(v, "v", kri)
-    k1 = inc(v.tensor_scalar(T.ri2[:], T.ri[:], 15, None, Op.bitwise_and), new())
-    need(v, "v", k1)
-    kmask = inc(v.tensor_scalar(T.mask[:], T.ri2[:], 0.0, None, Op.is_equal), new())
+    kj = inc(g.iota(T.jota[:, 0:512], [[1, 512]], -256, 0, allow_small_or_imprecise_dtypes=True), new())
+    inc(g.iota(T.jota[:, 512:E], [[2, E - 512]], 256, 0, allow_small_or_imprecise_dtypes=True), kj)
+    need(s, "s", kW, kD0)
+    kD = new()
+
+    def diagonals(rs):
+        for r in rs:
+            inc(s.activation(T.D[:, 128 * r + r:128 * r + 128:16], T.W[:, r:128:16], Act.Copy), kD)
+
+    diagonals(range(8))
 
     def turn(r, neg=False):
         o = 128 - 16 * (r % 8)
@@ -141,47 +140,53 @@ def rank_program(g, core, T, topo):
     ident = T.W[:, 0:128]
 
     def exchange(k, gather_v, gather_s, steps, gbuf, sbuf, lbuf, sign, started=(), clip=False):
-        gs, ms, es = {}, {}, [new(), new(), new()]
-        for who, what, i in steps:
+        ms, ready = {}, {}
+        for st in steps.split():
+            who, what, i = st[0], st[1], int(st[2])
             q = order[i]
+            out = lbuf if q == p else sbuf
+            direct = p * q % 8 == 0 and not clip
             if what == "g":
-                gs[i] = inc((gather_v if who == "v" else gather_s)(q, gbuf[:, col(q)]), new())
-                need(t, "t", gs[i], kW, *bank_read[i])
+                buf, gs = out if direct else gbuf, new()
+                for w, a, b in [("v", 0, CAP // 2), ("s", CAP // 2, CAP)] if who == "b" else [(who, 0, CAP)]:
+                    inc((gather_v if w == "v" else gather_s)(q, a, b, buf), gs)
+                if direct:
+                    ready[i] = gs
+                    continue
+                need(t, "t", gs, kW, *bank_read[i])
                 ms[i] = inc(t.matmul(banks[i][:, 0:128], turn(sign * p * q), gbuf[:, col(q)], i not in started, True), new())
-                continue
-            o = (lbuf if q == p else sbuf)[:, col(q)]
-            b = banks[i][:, 0:128]
-            if who == "v":
-                need(v, "v", ms[i])
-                ins = v.tensor_scalar(o, b, 63.0, -63.0, Op.min, Op.max) if clip else v.tensor_copy(o, b)
-            else:
-                need(s, "s", ms[i])
-                ins = s.activation(o, b, Act.Copy)
-            sem = es[0] if i < 2 else (es[2] if q == p else es[1])
-            inc(ins, sem)
-            bank_read[i] = [sem]
-        need(g, "g", es[0])
-        send(k, sbuf, lbuf, order[:2])
-        need(g, "g", es[1])
-        send(k, sbuf, lbuf, order[2:5])
-        return [es[2], "arr%d" % k]
+            elif not direct:
+                dst, b = out[:, col(q)], banks[i][:, 0:128]
+                if who == "v":
+                    need(v, "v", ms[i])
+                    ins = v.tensor_scalar(dst, b, 63.0, -63.0, Op.min, Op.max) if clip else v.tensor_copy(dst, b)
+                else:
+                    need(s, "s", ms[i])
+                    ins = s.activation(dst, b, Act.Copy)
+                ready[i] = inc(ins, new())
+                bank_read[i] = [ready[i]]
+        for i in range(N - 1):
+            need(g, "g", ready[i])
+            send(k, sbuf, lbuf, order[i])
+        return [ready[N - 1], "near%d" % k, "far%d" % k]
 
     def forward(k, window, ready, steps, started=(), clip=False):
-        def gv(q, o):
+        def gv(q, a, b, buf):
             need(v, "v", *ready)
-            return v.tensor_copy(o, window.indirect(T.sn16[:, 8 * q:8 * q + 8]))
+            return v.tensor_copy(buf[:, q * CAP + a:q * CAP + b], window.indirect(T.sn16[:, 8 * q + a // 16:8 * q + b // 16]))
 
-        def gs(q, o):
+        def gs(q, a, b, buf):
             need(s, "s", *ready)
-            return s.activation(o, window.indirect(T.sn16[:, 8 * q:8 * q + 8]), Act.Copy)
+            return s.activation(buf[:, q * CAP + a:q * CAP + b], window.indirect(T.sn16[:, 8 * q + a // 16:8 * q + b // 16]), Act.Copy)
         return exchange(2 * k, gv, gs, steps, T["gf%d" % k], T["sf%d" % k], T["lf%d" % k], 1, started, clip)
 
     need(v, "v", lsn)
     ksn = inc(v.tensor_copy(T.sn16[:], T.sn_i[:]), new())
-    here = forward(0, T.x_sb[:, 0:V], [ksn, lx],
-                   [("v", "g", 0), ("s", "g", 1), ("s", "o", 0), ("v", "g", 2), ("v", "o", 1), ("s", "g", 3), ("s", "o", 2),
-                    ("v", "g", 4), ("v", "o", 3), ("s", "o", 4), ("s", "g", 5), ("v", "o", 5)])
+    here = forward(0, T.x_sb[:, 0:V], [ksn, lx], F0)
 
+    diagonals(range(8, 16))
+    kxa = inc(s.activation(T.xa[:], T.x_sb[:], Act.Abs), new())
+    inc(s.activation(T.sx[:], T.x_sb[:], Act.Sign, 0.5, 1.0), kxa)
     need(v, "v", lpl)
     kpl = new()
     base, c0, o = [], 0, 0
@@ -193,33 +198,31 @@ def rank_program(g, core, T, topo):
         c0 += n // 16
     need(v, "v", kpl, kj, kwin)
     ksc = inc(v.tensor_copy(T.win[:].indirect(T.pl16[:, 0:36]), T.jota[:]), new())
-    need(v, "v", ksc, kmask)
-    km = [new(), new()]
+    need(t, "t", ksc, kD, *bank_read[4])
     for r in range(16):
-        inc(v.tensor_scalar(T.mk[:, 48 * r:48 * r + 48], T.win[:, r::16], T.mask[:, r:r + 1], None, Op.mult), km[r // 8])
-        if r % 8 == 7:
-            need(t, "t", kI, km[r // 8])
-            for u in range(r - 7, r + 1):
-                ins = t.matmul(banks[7][:, 0:48], T.I16[:], T.mk[:, 48 * u:48 * u + 48], u == 0, u == 15)
+        ins = t.matmul(banks[4][:, 0:48], T.D[:, 128 * r:128 * r + 128], T.win[:, r::16], r == 0, r == 15)
     kinvs = inc(ins, new())
-    need(v, "v", kinvs)
-    kinv = inc(v.tensor_copy(T.inv16[:], banks[7][:, 0:48]), new())
-    bank_read[7] = [kinv]
+    kinv, kb0, kvl, kWn = None, None, None, None
 
-    kvl = None
+    def place(h, e):
+        b = base[h] + e * HALF[h]
+        return slice(b, b + HALF[h]) if b < 512 else slice(512, XW, 2)
+
+    half = [slice(0, HALF[0]), slice(HALF[0], M)]
+    nb, vs, c = (VA, V - VA), [slice(0, VA), slice(VA, V)], VA // 16
+    bp, bg = banks[5], banks[3]
     for k in range(IT):
         last = k == IT - 1
-        lf, lb, sg = T["lf%d" % k], T["lb%d" % k], T["sg%d" % k]
+        lf, lb = T["lf%d" % k], T["lb%d" % k]
         A, G, S, X, par = [T["%s%d" % (n, k)] for n in ("A", "G", "S", "X", "par")]
         cols = [slice(base[h], base[h] + 4 * HALF[h]) for h in range(2)]
         lst = [T.pl16[:, base[h] // 16:base[h] // 16 + HALF[h] // 4] for h in range(2)]
         need(s, "s", kpl, *here)
         need(v, "v", kpl, *here)
-        kA = [inc(s.activation(A[:, cols[h]], lf[:].indirect(lst[h]), Act.Abs, 0.0, 2.0), new()) for h in range(2)]
+        kA = [inc(s.activation(A[:, cols[h]], lf[:].indirect(lst[h]), Act.Abs, 0.0, 4.0 if last else 2.0), new()) for h in range(2)]
         kG = [inc(v.tensor_scalar(G[:, cols[0]], lf[:].indirect(lst[0]), 0.0, 0.5, Op.is_ge, Op.subtract), new()),
               inc(s.activation(G[:, cols[1]], lf[:].indirect(lst[1]), Act.Sign, 0.5, 1.0), new())]
-        kpar, ksg = [], [new(), new()]
-        far, near = sorted(off), sorted(on + [p])
+        kpar = []
         for h, n in enumerate(HALF):
             need(t, "t", kG[h], *bank_read[6 + h])
             for e in range(4):
@@ -227,53 +230,96 @@ def rank_program(g, core, T, topo):
                 ins = t.matmul(banks[6 + h][:, 0:n], ident, G[:, b:b + n], e == 0, e == 3)
             kN = inc(ins, new())
             need(s, "s", kN)
-            ps = slice(0, n) if h == 0 else slice(HALF[0], M)
-            kpar.append(inc(s.activation(par[:, ps], banks[6 + h][:, 0:n], Act.Abs, 0.0, 1.0 if h == 0 else 0.5), new()))
+            kpar.append(inc(s.activation(par[:, half[h]], banks[6 + h][:, 0:n], Act.Abs, 0.0, 1.0 if h == 0 else 0.5), new()))
             bank_read[6 + h] = [kpar[h]]
-            for q in (far if h == 0 else near)[::3]:
-                w = slice(q * CAP, (q + 3) * CAP)
-                inc(s.activation(sg[:, w], lf[:, w], Act.Sign, 0.5, 1.0), ksg[h])
-        bp, bg = banks[5], banks[3]
-        kS = []
-        for h, n in enumerate(HALF):
-            b, o = base[h], (0, 2 * HALF[0])[h]
+        ksg = [new(), new()]
+        if last:
+            for h, w in enumerate((sorted(off), sorted(near))):
+                for q in w[::3]:
+                    w3 = slice(q * CAP, (q + 3) * CAP)
+                    inc(s.activation(T.sg1[:, w3], lf[:, w3], Act.Sign, 0.5, 1.0), ksg[h])
+        kS, kg, kX, o = [new(), new()], [new(), new()], new(), 256 if last else 0
+        k2 = list(kg)
+
+        def pairs(h):
+            n, b, a = HALF[h], base[h], (0, 2 * HALF[0])[h]
             need(v, "v", kA[h], *bank_read[5])
             kP = new()
-            inc(v.tensor_tensor(bp[:, o + n:o + 2 * n], A[:, b:b + n], A[:, b + 2 * n:b + 3 * n], Op.min), kP)
-            inc(v.tensor_tensor(bp[:, o:o + n], A[:, b + n:b + 2 * n], A[:, b + 3 * n:b + 4 * n], Op.min), kP)
+            inc(v.tensor_tensor(bp[:, a + n:a + 2 * n], A[:, b:b + n], A[:, b + 2 * n:b + 3 * n], Op.min), kP)
+            inc(v.tensor_tensor(bp[:, a:a + n], A[:, b + n:b + 2 * n], A[:, b + 3 * n:b + 4 * n], Op.min), kP)
+            return kP
+
+        def least(h, kP):
+            n, b, a = HALF[h], base[h], (0, 2 * HALF[0])[h]
             need(v, "v", kP)
-            kS.append(new())
-            inc(v.tensor_tensor(S[:, b:b + 2 * n], A[:, b + 2 * n:b + 4 * n], bp[:, o:o + 2 * n], Op.min), kS[h])
-            inc(v.tensor_tensor(S[:, b + 2 * n:b + 4 * n], A[:, b:b + 2 * n], bp[:, o:o + 2 * n], Op.min), kS[h])
-        kX = new()
-        for h, n in enumerate(HALF):
-            ps = slice(0, n) if h == 0 else slice(HALF[0], M)
+            inc(v.tensor_tensor(S[:, b:b + 2 * n], A[:, b + 2 * n:b + 4 * n], bp[:, a:a + 2 * n], Op.min), kS[h])
+            inc(v.tensor_tensor(S[:, b + 2 * n:b + 4 * n], A[:, b:b + 2 * n], bp[:, a:a + 2 * n], Op.min), kS[h])
+
+        def signs(h):
             need(v, "v", kpar[h], *bank_read[3])
-            kg = inc(v.tensor_scalar(bg[:, ps], par[:, ps], 1.0, 0.5, Op.not_equal, Op.subtract), new())
-            need(v, "v", kS[h], kg)
-            for e in range(4):
-                b = base[h] + e * n
-                inc(v.tensor_tensor(X[:, b:b + n], S[:, b:b + n], bg[:, ps], Op.mult), kX)
+            inc(v.tensor_scalar(bg[:, half[h]], par[:, half[h]], 1.0, 0.5, Op.not_equal, Op.subtract), kg[h])
+
+        def times_b0(h):
+            if last:
+                need(v, "v", kg[h], kb0)
+                k2[h] = inc(v.tensor_tensor(bg[:, o + half[h].start:o + half[h].stop], bg[:, half[h]], T.b0[:, half[h]], Op.mult), new())
+
+        def signed(h, e):
+            n, b = HALF[h], base[h] + e * HALF[h]
+            need(v, "v", kS[h], k2[h])
+            inc(v.tensor_tensor(X[:, place(h, e)], S[:, b:b + n], bg[:, o + half[h].start:o + half[h].stop], Op.mult), kX)
+
+        kP0 = pairs(0)
+        least(0, kP0)
+        kP1 = pairs(1)
+        signs(0)
+        least(1, kP1)
+        times_b0(0)
+        if last:
+            signs(1)
+        signed(0, 0)
+        signed(0, 1)
+        if not last:
+            signs(1)
+        times_b0(1)
+        signed(0, 2)
+        signed(0, 3)
+        for e in range(4):
+            signed(1, e)
         bank_read[5], bank_read[3] = list(kS), [kX]
+        if kinv is None:
+            need(v, "v", kinvs)
+            kinv = inc(v.tensor_scalar(T.inv16[:], banks[4][:, 0:48], 256.0, None, Op.add), new())
+            bank_read[4] = [kinv]
 
-        def gather_back(q, o):
-            need(v, "v", kX, kinv, ksg[0 if q in off else 1])
-            return v.tensor_tensor(o, X[:].indirect(T.inv16[:, 8 * q:8 * q + 8]), sg[:, col(q)], Op.mult)
+        def back_v(q, a, b, buf):
+            need(v, "v", kX, kinv)
+            w, i = slice(q * CAP + a, q * CAP + b), X[:].indirect(T.inv16[:, 8 * q + a // 16:8 * q + b // 16])
+            if not last:
+                return v.tensor_copy(buf[:, w], i)
+            need(v, "v", ksg[0 if q in off else 1])
+            return v.tensor_tensor(buf[:, w], i, T.sg1[:, w], Op.mult)
 
-        steps = []
-        for i in range(6):
-            steps += [("v", "g", i), ("s", "o", i)]
-        here = exchange(2 * k + 1, gather_back, None, steps, T["gb%d" % k], T["sb%d" % k], lb, -1)
+        def back_s(q, a, b, buf):
+            need(s, "s", kX, kinv)
+            return s.activation(buf[:, q * CAP + a:q * CAP + b], X[:].indirect(T.inv16[:, 8 * q + a // 16:8 * q + b // 16]), Act.Copy)
 
-        if kvl is None:
+        here = exchange(2 * k + 1, back_v, back_s, B1 if last else B0, T["gb%d" % k], T["sb%d" % k], lb, -1)
+
+        if not last:
+            kb0 = new()
+            for h in range(2):
+                inc(v.tensor_scalar(T.b0[:, half[h]], par[:, half[h]], 1.0, 0.5, Op.not_equal, Op.subtract), kb0)
+            kWn = inc(v.tensor_scalar(T.Wn[:], T.W[:], -1.0, None, Op.mult), new())
             need(v, "v", lvl)
-            kvl = inc(v.tensor_copy(T.vl16[:], T.vl_i[:]), new())
-            kvs, n = new(), (V - VA) // 16
+            kvl = new()
             for d in range(3):
-                inc(v.tensor_copy(T.vs16[:, n * d:n * d + n], T.vl_i[:, 12 * d + VA // 16:12 * d + 12]), kvs)
-        res, rs, nb = T.ysb if last else T.tot, T["rs%d" % k], V - VA
-        need(s, "s", kvs, *here)
-        krs = inc(s.activation(rs[:], lb[:].indirect(T.vs16[:, 0:12]), Act.Copy), new())
+                inc(v.tensor_copy(T.va16[:, c * d:c * (d + 1)], T.vl_i[:, 12 * d:12 * d + c]), kvl)
+                inc(v.tensor_copy(T.vs16[:, (12 - c) * d:(12 - c) * (d + 1)], T.vl_i[:, 12 * d + c:12 * d + 12]), kvl)
+        need(v, "v", kvl, *here)
+        need(s, "s", kvl, *here)
+        rs = T["rs%d" % k]
+        krs = inc(s.activation(rs[:], lb[:].indirect(T.vs16[:]), Act.Copy), new())
         started = []
 
         def minus(i):
@@ -282,34 +328,48 @@ def rank_program(g, core, T, topo):
             t.matmul(banks[i][:, 0:128], turn(p * q, True), lb[:, col(q)], True, False)
             started.append(i)
 
-        need(t, "t", *bank_read[6])
-        t.matmul(banks[6][:, 0:nb], ident, T.x_sb[:, VA:V], True, False)
+        def add_s():
+            need(t, "t", krs)
+            for d in range(3):
+                ins = t.matmul(banks[7][:, 0:nb[1]], ident, rs[:, nb[1] * d:nb[1] * (d + 1)], False, d == 2)
+            return inc(ins, new())
+
+        need(v, "v", kxa)
+        need(t, "t", kxa, *(bank_read[6] + bank_read[7]))
+        t.matmul(banks[7][:, 0:nb[1]], ident, T.xa[:, vs[1]], True, False)
+        w = [lb[:].indirect(T.va16[:, c * d:c * (d + 1)]) for d in range(3)]
         if not last:
             minus(0)
             minus(1)
-        need(t, "t", krs)
-        for d in range(3):
-            ins = t.matmul(banks[6][:, 0:nb], ident, rs[:, nb * d:nb * d + nb], False, d == 2)
-        kt = inc(ins, new())
-        need(s, "s", kt)
-        kTs = inc(s.activation(res[:, VA:V], banks[6][:, 0:nb], Act.Copy), new())
-        bank_read[6] = [kTs]
-        if not last:
+            kts = add_s()
             for i in range(2, 6):
                 minus(i)
-        need(v, "v", kvl, lx, *here)
-        prev, outs = T.x_sb, [T["ta%d" % k], T["tb%d" % k], res]
-        for d in range(3):
-            kT = inc(v.tensor_tensor(outs[d][:, 0:VA], lb[:].indirect(T.vl16[:, 12 * d:12 * d + VA // 16]), prev[:, 0:VA], Op.add),
-                     new())
-            prev = outs[d]
-            if d < 2:
-                need(v, "v", kT)
-        if not last:
-            here = forward(1, res[:, 0:V], [kT, kTs],
-                           [("v", "g", 0), ("s", "g", 1), ("s", "g", 2), ("v", "g", 4), ("v", "o", 0), ("v", "o", 1),
-                            ("s", "g", 3), ("v", "o", 2), ("s", "g", 5), ("v", "o", 4), ("v", "o", 3), ("v", "o", 5)], started, True)
-    need(sy, "sy", kT, kTs)
+            prev = T.xa
+            for d, r in enumerate((T.ta, T.tb, T.tot)):
+                kT = inc(v.tensor_tensor(r[:, 0:VA], w[d], prev[:, 0:VA], Op.add), new())
+                prev = r
+                if d < 2:
+                    need(v, "v", kT)
+            need(s, "s", kts)
+            kTs = inc(s.activation(T.tot[:, vs[1]], banks[7][:, 0:nb[1]], Act.Copy), new())
+            bank_read[7] = [kTs]
+            here = forward(1, T.tot[:, 0:V], [kT, kTs], F1, started, True)
+        else:
+            r0, r1, r2 = [T.ra[:, VA * d:VA * (d + 1)] for d in range(3)]
+            k0 = inc(v.tensor_tensor(r0, w[0], T.xa[:, vs[0]], Op.add), new())
+            kr2 = inc(v.tensor_copy(r2, w[2]), new())
+            need(v, "v", k0)
+            kr1 = inc(v.tensor_tensor(r1, w[1], r0, Op.add), new())
+            need(t, "t", kr2)
+            t.matmul(banks[6][:, 0:VA], ident, r2, True, False)
+            kts = add_s()
+            need(t, "t", kr1)
+            ktv = inc(t.matmul(banks[6][:, 0:VA], ident, r1, False, True), new())
+            ky = new()
+            for h, kk in ((1, kts), (0, ktv)):
+                need(v, "v", kk)
+                inc(v.tensor_tensor(T.ysb[:, vs[h]], banks[6 + h][:, 0:nb[h]], T.sx[:, vs[h]], Op.mult), ky)
+    need(sy, "sy", ky)
     inc(sy.dma_start(T.y[:], T.ysb[:]), new(), 16)
 
     for name in sorted(tot):

@@ -5,14 +5,15 @@ SL = N * CAP
 E = 576
 HALF = (80, 64)
 VA = 128
-XW = 640
+XW = 4 * HALF[0] + 5 * HALF[1]
 Act = ActivationFunctionType
 Op = AluOpType
 
-F0 = "bg0 vg1 sg2 vo0 so1 sg3 vg4 so2 vo3 sg5 so4 so5"
-B0 = "bg0 vg1 sg2 vo0 vo1 sg3 so2 vg4 vo3 sg5 so4 vo5"
-F1 = "bg0 sg1 sg2 vg4 vo0 vo1 sg3 vo2 sg5 vo4 vo3 vo5"
-B1 = "vg0 so0 vg1 so1 vg2 so2 vg3 so3 vg4 so4 vg5 so5"
+F0 = "bg0 sg2 vg1 sg3 vo0 sg4 so1 so2 so3 so4 bg5 so5"
+B0 = "vg1 bg0 sg2 vo1 sg3 so2 vg4 vo3 vg5 so4 vo5 vo0"
+F1 = "sg1 vg0 sg2 vo0 vg4 vo1 vo2 sg3 vo3 vo4 vg5 vo5"
+B1 = "vg0 vg1 so1 vg2 so2 vg3 vg4 so3 so4 so0 vg5 so5"
+CV = "P0 i P1 L0 s0 b0 L1 X00 X01 s1 X02 b1 X03 X10 X12 X13 X11"
 
 SCRATCH = {
     "x_sb": ("sbuf", [128, V], "bfloat16"),
@@ -22,6 +23,7 @@ SCRATCH = {
     "pl_i": ("sbuf", [128, 36], "int32"),
     "vl_i": ("sbuf", [128, 36], "int32"),
     "sn16": ("sbuf", [128, 48], "uint16"),
+    "pn16": ("sbuf", [128, 36], "uint16"),
     "pl16": ("sbuf", [128, 36], "uint16"),
     "va16": ("sbuf", [128, 3 * VA // 16], "uint16"),
     "vs16": ("sbuf", [128, 3 * (V - VA) // 16], "uint16"),
@@ -29,7 +31,8 @@ SCRATCH = {
     "ones": ("sbuf", [128, 256], "bfloat16"),
     "W": ("sbuf", [128, 256], "bfloat16"),
     "Wn": ("sbuf", [128, 256], "bfloat16"),
-    "D": ("sbuf", [128, 2048], "bfloat16"),
+    "Z": ("sbuf", [128, 144], "bfloat16"),
+    "cnt": ("sbuf", [128, HALF[0]], "bfloat16"),
     "jota": ("sbuf", [128, E], "bfloat16"),
     "win": ("sbuf", [128, SL], "bfloat16"),
     "ta": ("sbuf", [128, VA], "bfloat16"),
@@ -37,7 +40,7 @@ SCRATCH = {
     "tot": ("sbuf", [128, V], "bfloat16"),
     "ra": ("sbuf", [128, 3 * VA], "bfloat16"),
     "ysb": ("sbuf", [128, V], "float32"),
-    "b0": ("sbuf", [128, M], "float32"),
+    "b0": ("sbuf", [128, M], "bfloat16"),
     "sg1": ("sbuf", [128, SL], "bfloat16"),
 }
 for _k in range(IT):
@@ -56,7 +59,7 @@ for _k in range(IT):
 for _k in range(8):
     SCRATCH["bank%d" % _k] = ("psum", [128, 512], "float32")
 
-NS = 138
+NS = 141
 SEMAPHORES = ["near%d" % k for k in range(4)] + ["far%d" % k for k in range(4)] + ["sent"] + ["s%d" % k for k in range(NS)]
 
 
@@ -90,8 +93,20 @@ def rank_program(g, core, T, topo):
 
     near = [q for q in range(N) if topo.chip(cores[q]) == topo.chip(core)]
     far = [q for q in range(N) if q not in near]
+    one, two = (near, far) if 0 in near else (far, near)
+    mate = {}
+    for i in range(len(one)):
+        a, b = one[i], two[(i + 2) % len(two)]
+        mate[a], mate[b] = b, a
+    la = [i * mate[i] % 8 if i in one else 0 for i in range(N)]
+    lc = [-i * mate[i] % 8 if i in one else 0 for i in range(N)]
+
+    def shift(i, j):
+        return (i * j + lc[j] - la[i]) % 8
+
     i0 = near.index(p)
-    off = [far[(i + i0) % len(far)] for i in range(len(far))]
+    off = [mate[p]] + sorted([q for q in far if q != mate[p]],
+                             key=lambda q: (shift(p, q) != 0, (far.index(q) - far.index(mate[p])) % len(far)))
     on = [near[(i + i0) % len(near)] for i in range(1, len(near))]
     order = off + on + [p]
     fe = topo.engines(core, cores[off[0]])
@@ -107,29 +122,44 @@ def rank_program(g, core, T, topo):
     for k in range(4):
         tot["far%d" % k], tot["near%d" % k] = len(off) * len(fe), len(on) * len(ne)
 
-    lsn, lx, lpl, lvl = new(), new(), new(), new()
-    inc(sy.dma_start(T.sn_i[:], T.sn[:]), lsn, 16)
-    inc(s.dma_start(T.x_sb[:], T.x[:]), lx, 16)
-    inc(sy.dma_start(T.pl_i[:], T.pl[:]), lpl, 16)
-    inc(sy.dma_start(T.vl_i[:], T.vl[:]), lvl, 16)
+    def rows(r):
+        return [(0, 128, 0)] if r == 0 else [(0, 128 - 16 * r, 16 * r), (128 - 16 * r, 128, 0)]
+
+    def load(queue, dst, src, r):
+        name = new()
+        for a, b, to in rows(r):
+            inc(queue.dma_start(dst[to:to + b - a, :], src[a:b, :]), name, 16)
+        return name
+
+    lsn = load(sy, T.sn_i, T.sn, la[p])
+    lx = load(s, T.x_sb, T.x, la[p])
+    lpl = load(sy, T.pl_i, T.pl, lc[p])
+    lvl = load(sy, T.vl_i, T.vl, la[p])
 
     kones = inc(v.memset(T.ones[:], 1.0), new())
-    kD0 = inc(v.memset(T.D[:], 0.0), new())
+    kZ0 = inc(v.memset(T.Z[:], 0.0), new())
     kwin = inc(v.memset(T.win[:], 0.0), new())
-    for k in range(IT):
-        inc(v.memset(T["X%d" % k][:, 512:XW], 0.0), kwin)
+    kcnt = inc(g.iota(T.cnt[:], [[1, HALF[0]]], 0, 0, allow_small_or_imprecise_dtypes=True), new())
     need(g, "g", kones)
     kW = inc(g.affine_select(T.W[:], T.ones[:], [[0, 2], [-1, 128]], Op.is_equal, 0.0, 0, 1), new())
-    kj = inc(g.iota(T.jota[:, 0:512], [[1, 512]], -256, 0, allow_small_or_imprecise_dtypes=True), new())
-    inc(g.iota(T.jota[:, 512:E], [[2, E - 512]], 256, 0, allow_small_or_imprecise_dtypes=True), kj)
-    need(s, "s", kW, kD0)
-    kD = new()
 
-    def diagonals(rs):
-        for r in rs:
-            inc(s.activation(T.D[:, 128 * r + r:128 * r + 128:16], T.W[:, r:128:16], Act.Copy), kD)
+    base = [0, 4 * HALF[0]]
+    half = [slice(0, HALF[0]), slice(HALF[0], M)]
+    odd = XW - 2 * HALF[1]
 
-    diagonals(range(8))
+    def place(h, e):
+        b = base[h] + e * HALF[h]
+        return (b, 1) if b < odd else (odd + 2 * (b - odd), 2)
+
+    kj = new()
+    need(s, "s", kcnt)
+    for e in range(4):
+        for h in range(2):
+            b, st = place(h, e)
+            inc(s.activation(T.jota[:, e * M + half[h].start:e * M + half[h].stop], T.cnt[:, 0:HALF[h]], Act.Identity,
+                             float(b - 256), float(st)), kj)
+    need(s, "s", kW, kZ0)
+    kZ = inc(s.activation(T.Z[:, 15:128:16], T.W[:, 0:128:16], Act.Copy), new())
 
     def turn(r, neg=False):
         o = 128 - 16 * (r % 8)
@@ -139,24 +169,30 @@ def rank_program(g, core, T, topo):
     bank_read = [[] for _ in range(8)]
     ident = T.W[:, 0:128]
 
-    def exchange(k, gather_v, gather_s, steps, gbuf, sbuf, lbuf, sign, started=(), clip=False):
+    def exchange(k, gather_v, gather_s, steps, gbuf, sbuf, lbuf, forth, started=(), clip=False):
         ms, ready = {}, {}
         for st in steps.split():
             who, what, i = st[0], st[1], int(st[2])
             q = order[i]
             out = lbuf if q == p else sbuf
-            direct = p * q % 8 == 0 and not clip
+            r = shift(p, q) if forth else -shift(q, p)
+            direct = r == 0 and not clip
+            passed = clip and i == 0
             if what == "g":
                 buf, gs = out if direct else gbuf, new()
+                if passed:
+                    ms[i] = inc(v.tensor_tensor(buf[:, col(q)], T.tot[:, 0:V].indirect(T.sn16[:, 8 * q:8 * q + 8]),
+                                                T.lb0[:, col(q)], Op.subtract), gs)
+                    continue
                 for w, a, b in [("v", 0, CAP // 2), ("s", CAP // 2, CAP)] if who == "b" else [(who, 0, CAP)]:
                     inc((gather_v if w == "v" else gather_s)(q, a, b, buf), gs)
                 if direct:
                     ready[i] = gs
                     continue
                 need(t, "t", gs, kW, *bank_read[i])
-                ms[i] = inc(t.matmul(banks[i][:, 0:128], turn(sign * p * q), gbuf[:, col(q)], i not in started, True), new())
+                ms[i] = inc(t.matmul(banks[i][:, 0:128], turn(r), gbuf[:, col(q)], i not in started, True), new())
             elif not direct:
-                dst, b = out[:, col(q)], banks[i][:, 0:128]
+                dst, b = out[:, col(q)], gbuf[:, col(q)] if passed else banks[i][:, 0:128]
                 if who == "v":
                     need(v, "v", ms[i])
                     ins = v.tensor_scalar(dst, b, 63.0, -63.0, Op.min, Op.max) if clip else v.tensor_copy(dst, b)
@@ -164,7 +200,8 @@ def rank_program(g, core, T, topo):
                     need(s, "s", ms[i])
                     ins = s.activation(dst, b, Act.Copy)
                 ready[i] = inc(ins, new())
-                bank_read[i] = [ready[i]]
+                if not passed:
+                    bank_read[i] = [ready[i]]
         for i in range(N - 1):
             need(g, "g", ready[i])
             send(k, sbuf, lbuf, order[i])
@@ -178,50 +215,47 @@ def rank_program(g, core, T, topo):
         def gs(q, a, b, buf):
             need(s, "s", *ready)
             return s.activation(buf[:, q * CAP + a:q * CAP + b], window.indirect(T.sn16[:, 8 * q + a // 16:8 * q + b // 16]), Act.Copy)
-        return exchange(2 * k, gv, gs, steps, T["gf%d" % k], T["sf%d" % k], T["lf%d" % k], 1, started, clip)
+        return exchange(2 * k, gv, gs, steps, T["gf%d" % k], T["sf%d" % k], T["lf%d" % k], True, started, clip)
 
     need(v, "v", lsn)
     ksn = inc(v.tensor_copy(T.sn16[:], T.sn_i[:]), new())
     here = forward(0, T.x_sb[:, 0:V], [ksn, lx], F0)
 
-    diagonals(range(8, 16))
-    kxa = inc(s.activation(T.xa[:], T.x_sb[:], Act.Abs), new())
-    inc(s.activation(T.sx[:], T.x_sb[:], Act.Sign, 0.5, 1.0), kxa)
     need(v, "v", lpl)
+    kpn = inc(v.tensor_copy(T.pn16[:], T.pl_i[:]), new())
     kpl = new()
-    base, c0, o = [], 0, 0
+    o, c0 = 0, 0
     for n in HALF:
-        base.append(o * 16)
         for e in range(4):
             inc(v.tensor_copy(T.pl16[:, o:o + n // 16], T.pl_i[:, 9 * e + c0:9 * e + c0 + n // 16]), kpl)
             o += n // 16
         c0 += n // 16
-    need(v, "v", kpl, kj, kwin)
-    ksc = inc(v.tensor_copy(T.win[:].indirect(T.pl16[:, 0:36]), T.jota[:]), new())
-    need(t, "t", ksc, kD, *bank_read[4])
+    need(v, "v", kpn, kj, kwin)
+    ksc = inc(v.tensor_copy(T.win[:].indirect(T.pn16[:]), T.jota[:]), new())
+    need(t, "t", ksc, kZ, *bank_read[4])
     for r in range(16):
-        ins = t.matmul(banks[4][:, 0:48], T.D[:, 128 * r:128 * r + 128], T.win[:, r::16], r == 0, r == 15)
+        ins = t.matmul(banks[4][:, 0:48], T.Z[:, 15 - r:143 - r], T.win[:, r::16], r == 0, r == 15)
     kinvs = inc(ins, new())
-    kinv, kb0, kvl, kWn = None, None, None, None
-
-    def place(h, e):
-        b = base[h] + e * HALF[h]
-        return slice(b, b + HALF[h]) if b < 512 else slice(512, XW, 2)
-
-    half = [slice(0, HALF[0]), slice(HALF[0], M)]
+    kX0 = new()
+    for k in range(IT):
+        inc(v.memset(T["X%d" % k][:, odd:XW], 0.0), kX0)
+    need(s, "s", lx)
+    kxa = inc(s.activation(T.xa[:], T.x_sb[:], Act.Abs), new())
+    inc(s.activation(T.sx[:], T.x_sb[:], Act.Sign, 0.5, 1.0), kxa)
+    kinv = []
     nb, vs, c = (VA, V - VA), [slice(0, VA), slice(VA, V)], VA // 16
     bp, bg = banks[5], banks[3]
     for k in range(IT):
         last = k == IT - 1
         lf, lb = T["lf%d" % k], T["lb%d" % k]
-        A, G, S, X, par = [T["%s%d" % (n, k)] for n in ("A", "G", "S", "X", "par")]
+        A, G, S, X, par, rs = [T["%s%d" % (n, k)] for n in ("A", "G", "S", "X", "par", "rs")]
         cols = [slice(base[h], base[h] + 4 * HALF[h]) for h in range(2)]
         lst = [T.pl16[:, base[h] // 16:base[h] // 16 + HALF[h] // 4] for h in range(2)]
         need(s, "s", kpl, *here)
         need(v, "v", kpl, *here)
+        kG = [inc(v.tensor_scalar(G[:, cols[0]], lf[:].indirect(lst[0]), 0.0, 0.5, Op.is_ge, Op.subtract), new())]
         kA = [inc(s.activation(A[:, cols[h]], lf[:].indirect(lst[h]), Act.Abs, 0.0, 4.0 if last else 2.0), new()) for h in range(2)]
-        kG = [inc(v.tensor_scalar(G[:, cols[0]], lf[:].indirect(lst[0]), 0.0, 0.5, Op.is_ge, Op.subtract), new()),
-              inc(s.activation(G[:, cols[1]], lf[:].indirect(lst[1]), Act.Sign, 0.5, 1.0), new())]
+        kG.append(inc(s.activation(G[:, cols[1]], lf[:].indirect(lst[1]), Act.Sign, 0.5, 1.0), new()))
         kpar = []
         for h, n in enumerate(HALF):
             need(t, "t", kG[h], *bank_read[6 + h])
@@ -232,68 +266,48 @@ def rank_program(g, core, T, topo):
             need(s, "s", kN)
             kpar.append(inc(s.activation(par[:, half[h]], banks[6 + h][:, 0:n], Act.Abs, 0.0, 1.0 if h == 0 else 0.5), new()))
             bank_read[6 + h] = [kpar[h]]
-        ksg = [new(), new()]
+        ksg = []
         if last:
-            for h, w in enumerate((sorted(off), sorted(near))):
-                for q in w[::3]:
-                    w3 = slice(q * CAP, (q + 3) * CAP)
-                    inc(s.activation(T.sg1[:, w3], lf[:, w3], Act.Sign, 0.5, 1.0), ksg[h])
-        kS, kg, kX, o = [new(), new()], [new(), new()], new(), 256 if last else 0
-        k2 = list(kg)
-
-        def pairs(h):
+            for w in (sorted(off), sorted(near)):
+                w3 = slice(w[0] * CAP, (w[-1] + 1) * CAP)
+                ksg.append(inc(s.activation(T.sg1[:, w3], lf[:, w3], Act.Sign, 0.5, 1.0), new()))
+        kS, ko = [None, None], [None, None]
+        kX, o = new(), 256 if last else 0
+        for st in CV.split():
+            if st == "i":
+                if not kinv:
+                    need(v, "v", kinvs)
+                    kinv.append(inc(v.tensor_scalar(T.inv16[:], banks[4][:, 0:48], 256.0, None, Op.add), new()))
+                    bank_read[4] = [kinv[0]]
+                continue
+            h = int(st[1])
             n, b, a = HALF[h], base[h], (0, 2 * HALF[0])[h]
-            need(v, "v", kA[h], *bank_read[5])
-            kP = new()
-            inc(v.tensor_tensor(bp[:, a + n:a + 2 * n], A[:, b:b + n], A[:, b + 2 * n:b + 3 * n], Op.min), kP)
-            inc(v.tensor_tensor(bp[:, a:a + n], A[:, b + n:b + 2 * n], A[:, b + 3 * n:b + 4 * n], Op.min), kP)
-            return kP
-
-        def least(h, kP):
-            n, b, a = HALF[h], base[h], (0, 2 * HALF[0])[h]
-            need(v, "v", kP)
-            inc(v.tensor_tensor(S[:, b:b + 2 * n], A[:, b + 2 * n:b + 4 * n], bp[:, a:a + 2 * n], Op.min), kS[h])
-            inc(v.tensor_tensor(S[:, b + 2 * n:b + 4 * n], A[:, b:b + 2 * n], bp[:, a:a + 2 * n], Op.min), kS[h])
-
-        def signs(h):
-            need(v, "v", kpar[h], *bank_read[3])
-            inc(v.tensor_scalar(bg[:, half[h]], par[:, half[h]], 1.0, 0.5, Op.not_equal, Op.subtract), kg[h])
-
-        def times_b0(h):
-            if last:
-                need(v, "v", kg[h], kb0)
-                k2[h] = inc(v.tensor_tensor(bg[:, o + half[h].start:o + half[h].stop], bg[:, half[h]], T.b0[:, half[h]], Op.mult), new())
-
-        def signed(h, e):
-            n, b = HALF[h], base[h] + e * HALF[h]
-            need(v, "v", kS[h], k2[h])
-            inc(v.tensor_tensor(X[:, place(h, e)], S[:, b:b + n], bg[:, o + half[h].start:o + half[h].stop], Op.mult), kX)
-
-        kP0 = pairs(0)
-        least(0, kP0)
-        kP1 = pairs(1)
-        signs(0)
-        least(1, kP1)
-        times_b0(0)
-        if last:
-            signs(1)
-        signed(0, 0)
-        signed(0, 1)
-        if not last:
-            signs(1)
-        times_b0(1)
-        signed(0, 2)
-        signed(0, 3)
-        for e in range(4):
-            signed(1, e)
+            if st[0] == "P":
+                need(v, "v", kA[h], *bank_read[5])
+                kS[h] = new()
+                inc(v.tensor_tensor(bp[:, a + n:a + 2 * n], A[:, b:b + n], A[:, b + 2 * n:b + 3 * n], Op.min), kS[h])
+                inc(v.tensor_tensor(bp[:, a:a + n], A[:, b + n:b + 2 * n], A[:, b + 3 * n:b + 4 * n], Op.min), kS[h])
+            elif st[0] == "L":
+                need(v, "v", kS[h])
+                kS[h] = new()
+                inc(v.tensor_tensor(S[:, b:b + 2 * n], A[:, b + 2 * n:b + 4 * n], bp[:, a:a + 2 * n], Op.min), kS[h])
+                inc(v.tensor_tensor(S[:, b + 2 * n:b + 4 * n], A[:, b:b + 2 * n], bp[:, a:a + 2 * n], Op.min), kS[h])
+            elif st[0] == "s":
+                need(v, "v", kpar[h], *bank_read[3])
+                ko[h] = inc(v.tensor_scalar(bg[:, half[h]], par[:, half[h]], 1.0, 0.5, Op.not_equal, Op.subtract), new())
+            elif st[0] == "b":
+                if last:
+                    need(v, "v", ko[h], kb0)
+                    ko[h] = inc(v.tensor_tensor(bg[:, o + half[h].start:o + half[h].stop], bg[:, half[h]], T.b0[:, half[h]], Op.mult), new())
+            else:
+                pb, step = place(h, int(st[2]))
+                need(v, "v", ko[h], kS[h], kX0)
+                b += int(st[2]) * n
+                inc(v.tensor_tensor(X[:, pb:pb + n * step:step], S[:, b:b + n], bg[:, o + half[h].start:o + half[h].stop], Op.mult), kX)
         bank_read[5], bank_read[3] = list(kS), [kX]
-        if kinv is None:
-            need(v, "v", kinvs)
-            kinv = inc(v.tensor_scalar(T.inv16[:], banks[4][:, 0:48], 256.0, None, Op.add), new())
-            bank_read[4] = [kinv]
 
         def back_v(q, a, b, buf):
-            need(v, "v", kX, kinv)
+            need(v, "v", kX, *kinv)
             w, i = slice(q * CAP + a, q * CAP + b), X[:].indirect(T.inv16[:, 8 * q + a // 16:8 * q + b // 16])
             if not last:
                 return v.tensor_copy(buf[:, w], i)
@@ -301,31 +315,31 @@ def rank_program(g, core, T, topo):
             return v.tensor_tensor(buf[:, w], i, T.sg1[:, w], Op.mult)
 
         def back_s(q, a, b, buf):
-            need(s, "s", kX, kinv)
+            need(s, "s", kX, *kinv)
             return s.activation(buf[:, q * CAP + a:q * CAP + b], X[:].indirect(T.inv16[:, 8 * q + a // 16:8 * q + b // 16]), Act.Copy)
 
-        here = exchange(2 * k + 1, back_v, back_s, B1 if last else B0, T["gb%d" % k], T["sb%d" % k], lb, -1)
+        here = exchange(2 * k + 1, back_v, back_s, B1 if last else B0, T["gb%d" % k], T["sb%d" % k], lb, False)
 
         if not last:
             kb0 = new()
             for h in range(2):
                 inc(v.tensor_scalar(T.b0[:, half[h]], par[:, half[h]], 1.0, 0.5, Op.not_equal, Op.subtract), kb0)
+            need(v, "v", kW)
             kWn = inc(v.tensor_scalar(T.Wn[:], T.W[:], -1.0, None, Op.mult), new())
             need(v, "v", lvl)
             kvl = new()
             for d in range(3):
                 inc(v.tensor_copy(T.va16[:, c * d:c * (d + 1)], T.vl_i[:, 12 * d:12 * d + c]), kvl)
                 inc(v.tensor_copy(T.vs16[:, (12 - c) * d:(12 - c) * (d + 1)], T.vl_i[:, 12 * d + c:12 * d + 12]), kvl)
-        need(v, "v", kvl, *here)
+        need(v, "v", kvl, kxa, *here)
         need(s, "s", kvl, *here)
-        rs = T["rs%d" % k]
         krs = inc(s.activation(rs[:], lb[:].indirect(T.vs16[:]), Act.Copy), new())
         started = []
 
         def minus(i):
             q = order[i]
             need(t, "t", kWn, *(bank_read[i] + here))
-            t.matmul(banks[i][:, 0:128], turn(p * q, True), lb[:, col(q)], True, False)
+            t.matmul(banks[i][:, 0:128], turn(shift(p, q), True), lb[:, col(q)], True, False)
             started.append(i)
 
         def add_s():
@@ -334,15 +348,14 @@ def rank_program(g, core, T, topo):
                 ins = t.matmul(banks[7][:, 0:nb[1]], ident, rs[:, nb[1] * d:nb[1] * (d + 1)], False, d == 2)
             return inc(ins, new())
 
-        need(v, "v", kxa)
         need(t, "t", kxa, *(bank_read[6] + bank_read[7]))
         t.matmul(banks[7][:, 0:nb[1]], ident, T.xa[:, vs[1]], True, False)
         w = [lb[:].indirect(T.va16[:, c * d:c * (d + 1)]) for d in range(3)]
         if not last:
-            minus(0)
             minus(1)
+            minus(2)
             kts = add_s()
-            for i in range(2, 6):
+            for i in range(3, 6):
                 minus(i)
             prev = T.xa
             for d, r in enumerate((T.ta, T.tb, T.tot)):
@@ -353,6 +366,7 @@ def rank_program(g, core, T, topo):
             need(s, "s", kts)
             kTs = inc(s.activation(T.tot[:, vs[1]], banks[7][:, 0:nb[1]], Act.Copy), new())
             bank_read[7] = [kTs]
+            need(v, "v", kT, kTs)
             here = forward(1, T.tot[:, 0:V], [kT, kTs], F1, started, True)
         else:
             r0, r1, r2 = [T.ra[:, VA * d:VA * (d + 1)] for d in range(3)]
@@ -370,7 +384,9 @@ def rank_program(g, core, T, topo):
                 need(v, "v", kk)
                 inc(v.tensor_tensor(T.ysb[:, vs[h]], banks[6 + h][:, 0:nb[h]], T.sx[:, vs[h]], Op.mult), ky)
     need(sy, "sy", ky)
-    inc(sy.dma_start(T.y[:], T.ysb[:]), new(), 16)
+    ly = new()
+    for a, b, to in rows(la[p]):
+        inc(sy.dma_start(T.y[a:b, :], T.ysb[to:to + b - a, :]), ly, 16)
 
     for name in sorted(tot):
         if max([n for (_, m), n in seen.items() if m == name] + [0]) < tot[name]:

from concourse.mybir import AluOpType, ActivationFunctionType

N, CAP, V, M, IT = 6, 128, 192, 144, 2
SL = N * CAP
E = 576
HALF = (80, 64)
VA = 128
XW = 4 * HALF[0] + 5 * HALF[1]
Act = ActivationFunctionType
Op = AluOpType

F0 = "bg0 sg2 vg1 sg3 vo0 sg4 so1 so2 so3 so4 bg5 so5"
B0 = "vg1 bg0 sg2 vo1 sg3 so2 vg4 vo3 vg5 so4 vo5 vo0"
F1 = "sg1 vg0 sg2 vo0 vg4 vo1 vo2 sg3 vo3 vo4 vg5 vo5"
B1 = "vg0 vg1 so1 vg2 so2 vg3 vg4 so3 so4 so0 vg5 so5"
CV = "P0 i P1 L0 s0 b0 L1 X00 X01 s1 X02 b1 X03 X10 X12 X13 X11"

SCRATCH = {
    "x_sb": ("sbuf", [128, V], "bfloat16"),
    "xa": ("sbuf", [128, V], "bfloat16"),
    "sx": ("sbuf", [128, V], "bfloat16"),
    "sn_i": ("sbuf", [128, 48], "int32"),
    "pl_i": ("sbuf", [128, 36], "int32"),
    "vl_i": ("sbuf", [128, 36], "int32"),
    "sn16": ("sbuf", [128, 48], "uint16"),
    "pn16": ("sbuf", [128, 36], "uint16"),
    "pl16": ("sbuf", [128, 36], "uint16"),
    "va16": ("sbuf", [128, 3 * VA // 16], "uint16"),
    "vs16": ("sbuf", [128, 3 * (V - VA) // 16], "uint16"),
    "inv16": ("sbuf", [128, 48], "uint16"),
    "ones": ("sbuf", [128, 256], "bfloat16"),
    "W": ("sbuf", [128, 256], "bfloat16"),
    "Wn": ("sbuf", [128, 256], "bfloat16"),
    "Z": ("sbuf", [128, 144], "bfloat16"),
    "cnt": ("sbuf", [128, HALF[0]], "bfloat16"),
    "jota": ("sbuf", [128, E], "bfloat16"),
    "win": ("sbuf", [128, SL], "bfloat16"),
    "ta": ("sbuf", [128, VA], "bfloat16"),
    "tb": ("sbuf", [128, VA], "bfloat16"),
    "tot": ("sbuf", [128, V], "bfloat16"),
    "ra": ("sbuf", [128, 3 * VA], "bfloat16"),
    "ysb": ("sbuf", [128, V], "float32"),
    "b0": ("sbuf", [128, M], "bfloat16"),
    "sg1": ("sbuf", [128, SL], "bfloat16"),
}
for _k in range(IT):
    SCRATCH["gf%d" % _k] = ("sbuf", [128, SL], "bfloat16")
    SCRATCH["sf%d" % _k] = ("sbuf", [128, SL], "bfloat16")
    SCRATCH["lf%d" % _k] = ("sbuf", [128, SL], "bfloat16")
    SCRATCH["gb%d" % _k] = ("sbuf", [128, SL], "bfloat16")
    SCRATCH["sb%d" % _k] = ("sbuf", [128, SL], "bfloat16")
    SCRATCH["lb%d" % _k] = ("sbuf", [128, SL], "bfloat16")
    SCRATCH["A%d" % _k] = ("sbuf", [128, E], "bfloat16")
    SCRATCH["G%d" % _k] = ("sbuf", [128, E], "bfloat16")
    SCRATCH["S%d" % _k] = ("sbuf", [128, E], "bfloat16")
    SCRATCH["X%d" % _k] = ("sbuf", [128, XW], "bfloat16")
    SCRATCH["par%d" % _k] = ("sbuf", [128, M], "bfloat16")
    SCRATCH["rs%d" % _k] = ("sbuf", [128, 3 * (V - VA)], "bfloat16")
for _k in range(8):
    SCRATCH["bank%d" % _k] = ("psum", [128, 512], "float32")

NS = 141
SEMAPHORES = ["near%d" % k for k in range(4)] + ["far%d" % k for k in range(4)] + ["sent"] + ["s%d" % k for k in range(NS)]


def rank_program(g, core, T, topo):
    p = T.rank_of(core)
    if p is None:
        return
    cores = list(T.cores)
    v, s, t, sy = g.vector, g.scalar, g.tensor, g.sync

    tot, seen, nxt = {}, {}, [0]

    def new():
        n = "s%d" % nxt[0]
        nxt[0] += 1
        return n

    def inc(ins, name, n=1):
        ins.then_inc(T.sem[name], n)
        tot[name] = tot.get(name, 0) + n
        return name

    def need(queue, qname, *names):
        for name in names:
            if seen.get((qname, name), 0) < tot[name]:
                queue.wait_ge(T.sem[name], tot[name])
                seen[(qname, name)] = tot[name]

    def col(q):
        return slice(q * CAP, (q + 1) * CAP)

    near = [q for q in range(N) if topo.chip(cores[q]) == topo.chip(core)]
    far = [q for q in range(N) if q not in near]
    one, two = (near, far) if 0 in near else (far, near)
    mate = {}
    for i in range(len(one)):
        a, b = one[i], two[(i + 2) % len(two)]
        mate[a], mate[b] = b, a
    la = [i * mate[i] % 8 if i in one else 0 for i in range(N)]
    lc = [-i * mate[i] % 8 if i in one else 0 for i in range(N)]

    def shift(i, j):
        return (i * j + lc[j] - la[i]) % 8

    i0 = near.index(p)
    off = [mate[p]] + sorted([q for q in far if q != mate[p]],
                             key=lambda q: (shift(p, q) != 0, (far.index(q) - far.index(mate[p])) % len(far)))
    on = [near[(i + i0) % len(near)] for i in range(1, len(near))]
    order = off + on + [p]
    fe = topo.engines(core, cores[off[0]])
    ne = [e for e in topo.engines(core, cores[on[0]]) if e not in fe]

    def send(k, src, dst, q):
        es = fe if q in off else ne
        rid, pid, _ = topo.addr(cores[q])
        g.remote_dma(dst[:, col(p)], src[:, col(q)], T.sem["%s%d" % ("far" if q in off else "near", k)], T.sem["sent"],
                     pid, rid, sum(1 << e for e in es))
        tot["sent"] = tot.get("sent", 0) + len(es)

    for k in range(4):
        tot["far%d" % k], tot["near%d" % k] = len(off) * len(fe), len(on) * len(ne)

    def rows(r):
        return [(0, 128, 0)] if r == 0 else [(0, 128 - 16 * r, 16 * r), (128 - 16 * r, 128, 0)]

    def load(queue, dst, src, r):
        name = new()
        for a, b, to in rows(r):
            inc(queue.dma_start(dst[to:to + b - a, :], src[a:b, :]), name, 16)
        return name

    lsn = load(sy, T.sn_i, T.sn, la[p])
    lx = load(s, T.x_sb, T.x, la[p])
    lpl = load(sy, T.pl_i, T.pl, lc[p])
    lvl = load(sy, T.vl_i, T.vl, la[p])

    kones = inc(v.memset(T.ones[:], 1.0), new())
    kZ0 = inc(v.memset(T.Z[:], 0.0), new())
    kwin = inc(v.memset(T.win[:], 0.0), new())
    kcnt = inc(g.iota(T.cnt[:], [[1, HALF[0]]], 0, 0, allow_small_or_imprecise_dtypes=True), new())
    need(g, "g", kones)
    kW = inc(g.affine_select(T.W[:], T.ones[:], [[0, 2], [-1, 128]], Op.is_equal, 0.0, 0, 1), new())

    base = [0, 4 * HALF[0]]
    half = [slice(0, HALF[0]), slice(HALF[0], M)]
    odd = XW - 2 * HALF[1]

    def place(h, e):
        b = base[h] + e * HALF[h]
        return (b, 1) if b < odd else (odd + 2 * (b - odd), 2)

    kj = new()
    need(s, "s", kcnt)
    for e in range(4):
        for h in range(2):
            b, st = place(h, e)
            inc(s.activation(T.jota[:, e * M + half[h].start:e * M + half[h].stop], T.cnt[:, 0:HALF[h]], Act.Identity,
                             float(b - 256), float(st)), kj)
    need(s, "s", kW, kZ0)
    kZ = inc(s.activation(T.Z[:, 15:128:16], T.W[:, 0:128:16], Act.Copy), new())

    def turn(r, neg=False):
        o = 128 - 16 * (r % 8)
        return (T.Wn if neg else T.W)[:, o:o + 128]

    banks = [T["bank%d" % i] for i in range(8)]
    bank_read = [[] for _ in range(8)]
    ident = T.W[:, 0:128]

    def exchange(k, gather_v, gather_s, steps, gbuf, sbuf, lbuf, forth, started=(), clip=False):
        ms, ready = {}, {}
        for st in steps.split():
            who, what, i = st[0], st[1], int(st[2])
            q = order[i]
            out = lbuf if q == p else sbuf
            r = shift(p, q) if forth else -shift(q, p)
            direct = r == 0 and not clip
            passed = clip and i == 0
            if what == "g":
                buf, gs = out if direct else gbuf, new()
                if passed:
                    ms[i] = inc(v.tensor_tensor(buf[:, col(q)], T.tot[:, 0:V].indirect(T.sn16[:, 8 * q:8 * q + 8]),
                                                T.lb0[:, col(q)], Op.subtract), gs)
                    continue
                for w, a, b in [("v", 0, CAP // 2), ("s", CAP // 2, CAP)] if who == "b" else [(who, 0, CAP)]:
                    inc((gather_v if w == "v" else gather_s)(q, a, b, buf), gs)
                if direct:
                    ready[i] = gs
                    continue
                need(t, "t", gs, kW, *bank_read[i])
                ms[i] = inc(t.matmul(banks[i][:, 0:128], turn(r), gbuf[:, col(q)], i not in started, True), new())
            elif not direct:
                dst, b = out[:, col(q)], gbuf[:, col(q)] if passed else banks[i][:, 0:128]
                if who == "v":
                    need(v, "v", ms[i])
                    ins = v.tensor_scalar(dst, b, 63.0, -63.0, Op.min, Op.max) if clip else v.tensor_copy(dst, b)
                else:
                    need(s, "s", ms[i])
                    ins = s.activation(dst, b, Act.Copy)
                ready[i] = inc(ins, new())
                if not passed:
                    bank_read[i] = [ready[i]]
        for i in range(N - 1):
            need(g, "g", ready[i])
            send(k, sbuf, lbuf, order[i])
        return [ready[N - 1], "near%d" % k, "far%d" % k]

    def forward(k, window, ready, steps, started=(), clip=False):
        def gv(q, a, b, buf):
            need(v, "v", *ready)
            return v.tensor_copy(buf[:, q * CAP + a:q * CAP + b], window.indirect(T.sn16[:, 8 * q + a // 16:8 * q + b // 16]))

        def gs(q, a, b, buf):
            need(s, "s", *ready)
            return s.activation(buf[:, q * CAP + a:q * CAP + b], window.indirect(T.sn16[:, 8 * q + a // 16:8 * q + b // 16]), Act.Copy)
        return exchange(2 * k, gv, gs, steps, T["gf%d" % k], T["sf%d" % k], T["lf%d" % k], True, started, clip)

    need(v, "v", lsn)
    ksn = inc(v.tensor_copy(T.sn16[:], T.sn_i[:]), new())
    here = forward(0, T.x_sb[:, 0:V], [ksn, lx], F0)

    need(v, "v", lpl)
    kpn = inc(v.tensor_copy(T.pn16[:], T.pl_i[:]), new())
    kpl = new()
    o, c0 = 0, 0
    for n in HALF:
        for e in range(4):
            inc(v.tensor_copy(T.pl16[:, o:o + n // 16], T.pl_i[:, 9 * e + c0:9 * e + c0 + n // 16]), kpl)
            o += n // 16
        c0 += n // 16
    need(v, "v", kpn, kj, kwin)
    ksc = inc(v.tensor_copy(T.win[:].indirect(T.pn16[:]), T.jota[:]), new())
    need(t, "t", ksc, kZ, *bank_read[4])
    for r in range(16):
        ins = t.matmul(banks[4][:, 0:48], T.Z[:, 15 - r:143 - r], T.win[:, r::16], r == 0, r == 15)
    kinvs = inc(ins, new())
    kX0 = new()
    for k in range(IT):
        inc(v.memset(T["X%d" % k][:, odd:XW], 0.0), kX0)
    need(s, "s", lx)
    kxa = inc(s.activation(T.xa[:], T.x_sb[:], Act.Abs), new())
    inc(s.activation(T.sx[:], T.x_sb[:], Act.Sign, 0.5, 1.0), kxa)
    kinv = []
    nb, vs, c = (VA, V - VA), [slice(0, VA), slice(VA, V)], VA // 16
    bp, bg = banks[5], banks[3]
    for k in range(IT):
        last = k == IT - 1
        lf, lb = T["lf%d" % k], T["lb%d" % k]
        A, G, S, X, par, rs = [T["%s%d" % (n, k)] for n in ("A", "G", "S", "X", "par", "rs")]
        cols = [slice(base[h], base[h] + 4 * HALF[h]) for h in range(2)]
        lst = [T.pl16[:, base[h] // 16:base[h] // 16 + HALF[h] // 4] for h in range(2)]
        need(s, "s", kpl, *here)
        need(v, "v", kpl, *here)
        kG = [inc(v.tensor_scalar(G[:, cols[0]], lf[:].indirect(lst[0]), 0.0, 0.5, Op.is_ge, Op.subtract), new())]
        kA = [inc(s.activation(A[:, cols[h]], lf[:].indirect(lst[h]), Act.Abs, 0.0, 4.0 if last else 2.0), new()) for h in range(2)]
        kG.append(inc(s.activation(G[:, cols[1]], lf[:].indirect(lst[1]), Act.Sign, 0.5, 1.0), new()))
        kpar = []
        for h, n in enumerate(HALF):
            need(t, "t", kG[h], *bank_read[6 + h])
            for e in range(4):
                b = base[h] + e * n
                ins = t.matmul(banks[6 + h][:, 0:n], ident, G[:, b:b + n], e == 0, e == 3)
            kN = inc(ins, new())
            need(s, "s", kN)
            kpar.append(inc(s.activation(par[:, half[h]], banks[6 + h][:, 0:n], Act.Abs, 0.0, 1.0 if h == 0 else 0.5), new()))
            bank_read[6 + h] = [kpar[h]]
        ksg = []
        if last:
            for w in (sorted(off), sorted(near)):
                w3 = slice(w[0] * CAP, (w[-1] + 1) * CAP)
                ksg.append(inc(s.activation(T.sg1[:, w3], lf[:, w3], Act.Sign, 0.5, 1.0), new()))
        kS, ko = [None, None], [None, None]
        kX, o = new(), 256 if last else 0
        for st in CV.split():
            if st == "i":
                if not kinv:
                    need(v, "v", kinvs)
                    kinv.append(inc(v.tensor_scalar(T.inv16[:], banks[4][:, 0:48], 256.0, None, Op.add), new()))
                    bank_read[4] = [kinv[0]]
                continue
            h = int(st[1])
            n, b, a = HALF[h], base[h], (0, 2 * HALF[0])[h]
            if st[0] == "P":
                need(v, "v", kA[h], *bank_read[5])
                kS[h] = new()
                inc(v.tensor_tensor(bp[:, a + n:a + 2 * n], A[:, b:b + n], A[:, b + 2 * n:b + 3 * n], Op.min), kS[h])
                inc(v.tensor_tensor(bp[:, a:a + n], A[:, b + n:b + 2 * n], A[:, b + 3 * n:b + 4 * n], Op.min), kS[h])
            elif st[0] == "L":
                need(v, "v", kS[h])
                kS[h] = new()
                inc(v.tensor_tensor(S[:, b:b + 2 * n], A[:, b + 2 * n:b + 4 * n], bp[:, a:a + 2 * n], Op.min), kS[h])
                inc(v.tensor_tensor(S[:, b + 2 * n:b + 4 * n], A[:, b:b + 2 * n], bp[:, a:a + 2 * n], Op.min), kS[h])
            elif st[0] == "s":
                need(v, "v", kpar[h], *bank_read[3])
                ko[h] = inc(v.tensor_scalar(bg[:, half[h]], par[:, half[h]], 1.0, 0.5, Op.not_equal, Op.subtract), new())
            elif st[0] == "b":
                if last:
                    need(v, "v", ko[h], kb0)
                    ko[h] = inc(v.tensor_tensor(bg[:, o + half[h].start:o + half[h].stop], bg[:, half[h]], T.b0[:, half[h]], Op.mult), new())
            else:
                pb, step = place(h, int(st[2]))
                need(v, "v", ko[h], kS[h], kX0)
                b += int(st[2]) * n
                inc(v.tensor_tensor(X[:, pb:pb + n * step:step], S[:, b:b + n], bg[:, o + half[h].start:o + half[h].stop], Op.mult), kX)
        bank_read[5], bank_read[3] = list(kS), [kX]

        def back_v(q, a, b, buf):
            need(v, "v", kX, *kinv)
            w, i = slice(q * CAP + a, q * CAP + b), X[:].indirect(T.inv16[:, 8 * q + a // 16:8 * q + b // 16])
            if not last:
                return v.tensor_copy(buf[:, w], i)
            need(v, "v", ksg[0 if q in off else 1])
            return v.tensor_tensor(buf[:, w], i, T.sg1[:, w], Op.mult)

        def back_s(q, a, b, buf):
            need(s, "s", kX, *kinv)
            return s.activation(buf[:, q * CAP + a:q * CAP + b], X[:].indirect(T.inv16[:, 8 * q + a // 16:8 * q + b // 16]), Act.Copy)

        here = exchange(2 * k + 1, back_v, back_s, B1 if last else B0, T["gb%d" % k], T["sb%d" % k], lb, False)

        if not last:
            kb0 = new()
            for h in range(2):
                inc(v.tensor_scalar(T.b0[:, half[h]], par[:, half[h]], 1.0, 0.5, Op.not_equal, Op.subtract), kb0)
            need(v, "v", kW)
            kWn = inc(v.tensor_scalar(T.Wn[:], T.W[:], -1.0, None, Op.mult), new())
            need(v, "v", lvl)
            kvl = new()
            for d in range(3):
                inc(v.tensor_copy(T.va16[:, c * d:c * (d + 1)], T.vl_i[:, 12 * d:12 * d + c]), kvl)
                inc(v.tensor_copy(T.vs16[:, (12 - c) * d:(12 - c) * (d + 1)], T.vl_i[:, 12 * d + c:12 * d + 12]), kvl)
        need(v, "v", kvl, kxa, *here)
        need(s, "s", kvl, *here)
        krs = inc(s.activation(rs[:], lb[:].indirect(T.vs16[:]), Act.Copy), new())
        started = []

        def minus(i):
            q = order[i]
            need(t, "t", kWn, *(bank_read[i] + here))
            t.matmul(banks[i][:, 0:128], turn(shift(p, q), True), lb[:, col(q)], True, False)
            started.append(i)

        def add_s():
            need(t, "t", krs)
            for d in range(3):
                ins = t.matmul(banks[7][:, 0:nb[1]], ident, rs[:, nb[1] * d:nb[1] * (d + 1)], False, d == 2)
            return inc(ins, new())

        need(t, "t", kxa, *(bank_read[6] + bank_read[7]))
        t.matmul(banks[7][:, 0:nb[1]], ident, T.xa[:, vs[1]], True, False)
        w = [lb[:].indirect(T.va16[:, c * d:c * (d + 1)]) for d in range(3)]
        if not last:
            minus(1)
            minus(2)
            kts = add_s()
            for i in range(3, 6):
                minus(i)
            prev = T.xa
            for d, r in enumerate((T.ta, T.tb, T.tot)):
                kT = inc(v.tensor_tensor(r[:, 0:VA], w[d], prev[:, 0:VA], Op.add), new())
                prev = r
                if d < 2:
                    need(v, "v", kT)
            need(s, "s", kts)
            kTs = inc(s.activation(T.tot[:, vs[1]], banks[7][:, 0:nb[1]], Act.Copy), new())
            bank_read[7] = [kTs]
            need(v, "v", kT, kTs)
            here = forward(1, T.tot[:, 0:V], [kT, kTs], F1, started, True)
        else:
            r0, r1, r2 = [T.ra[:, VA * d:VA * (d + 1)] for d in range(3)]
            k0 = inc(v.tensor_tensor(r0, w[0], T.xa[:, vs[0]], Op.add), new())
            kr2 = inc(v.tensor_copy(r2, w[2]), new())
            need(v, "v", k0)
            kr1 = inc(v.tensor_tensor(r1, w[1], r0, Op.add), new())
            need(t, "t", kr2)
            t.matmul(banks[6][:, 0:VA], ident, r2, True, False)
            kts = add_s()
            need(t, "t", kr1)
            ktv = inc(t.matmul(banks[6][:, 0:VA], ident, r1, False, True), new())
            ky = new()
            for h, kk in ((1, kts), (0, ktv)):
                need(v, "v", kk)
                inc(v.tensor_tensor(T.ysb[:, vs[h]], banks[6 + h][:, 0:nb[h]], T.sx[:, vs[h]], Op.mult), ky)
    need(sy, "sy", ky)
    ly = new()
    for a, b, to in rows(la[p]):
        inc(sy.dma_start(T.y[a:b, :], T.ysb[to:to + b - a, :]), ly, 16)

    for name in sorted(tot):
        if max([n for (_, m), n in seen.items() if m == name] + [0]) < tot[name]:
            need(g, "g", name)
